import numpy as np, ml_dtypes
CORES = [24,25,26,27,28,29,30,31]
N = 8
BF = ml_dtypes.bfloat16
def gentries(a):
    return np.ascontiguousarray(a.reshape(8, 16, -1).transpose(0, 2, 1)).reshape(8, -1)
def gtable(e):
    e = np.asarray(e); return np.ascontiguousarray(e.reshape(8, -1, 16).transpose(0, 2, 1)).reshape(128, -1).astype(np.int32)
M, D, B, RO, Q = 256, 1024, 1024, 3, 5
NV = 16 * M
def parts(rng):
    v = rng.integers(0, 256, (N, 8, 16, NV)); a = rng.integers(0, NV, (N, 8, 16, D)); l = rng.integers(0, NV, (N, 8, 16, B))
    z = rng.integers(0, 256, (N, 8, 16, M)); c = rng.integers(0, B, (N, 8, M)); ka = rng.integers(0, 4096, (N, 8, 16))
    th = rng.integers(1150, 1450, (N, 8, 1)) + rng.integers(-150, 151, (N, 8, 16))
    return v, a, l, z, c, ka, th
def pack(v, a, l, z, c, ka, th):
    return {"vf": np.ascontiguousarray(v.reshape(N, 128, NV)).astype(np.float32).astype(BF), "ad": np.ascontiguousarray(a.reshape(N, 128, D)).astype(np.int32),
            "le": np.ascontiguousarray(l.reshape(N, 128, B)).astype(np.int32), "z0": np.ascontiguousarray(z.reshape(N, 128, M)).astype(np.float32).astype(BF),
            "cb": np.stack([gtable(x) for x in c]), "ka": ka.reshape(N, 128, 1).astype(np.int32), "th": th.reshape(N, 128, 1).astype(np.int32)}
def setup_inputs(rng):
    return pack(*parts(rng))
def setup_inputs_spread(rng):
    def uneven(n, *shape):
        v = np.minimum((n * rng.random((N, 8) + shape) ** 3).astype(np.int64), n - 1)
        up = (np.arange(8) % 2 == 1).reshape((1, 8) + (1,) * len(shape))
        return np.where(up, n - 1 - v, v)
    def sizes(n):
        return np.minimum((np.exp2(8.5 * rng.random((N, 8, 1, n))) * rng.random((N, 8, 16, n))).astype(np.int64), 255)
    th = np.minimum((4081 * rng.random((N, 8, 16)) ** 2.5).astype(np.int64), 4080)
    return pack(sizes(NV), uneven(NV, 16, D), uneven(NV, 16, B), sizes(M), uneven(B, M), uneven(4096, 16), th)
def setup_inputs_ends(rng):
    def halves(n):
        e = rng.random((N, 8, 16, n)) < 0.5; a = rng.random((N, 8, 1, n)) < 0.5
        return np.where(rng.random((N, 8, 1, n)) < 0.5, a, e).astype(np.int64)
    def coin(*shape):
        return (rng.random((N, 8) + shape) < 0.5).astype(np.int64)
    v = 255 * halves(NV); v[:, 1::2, :, 0] = 0; v[:, 1::2, :, NV - 1] = 255; v[:, 0, :, 0] = 255; v[:, 0, :, NV - 1] = 0
    top = np.zeros(16, np.int64); top[np.array([0, 1, 2, 6, 9])] = 255
    z = np.where(rng.random((N, 8, 1, M)) < 0.15, top[:, None], 255 * halves(M)); z[..., M - 1] = top; z[..., M - 2] = 255; z[..., 0] = 0
    c = (B - 1) * coin(M); c[..., M - 1] = B - 1; c[..., 0] = 0
    l = (NV - 1) * coin(16, B); l[:, :, 15, B - 1] = NV - 1; l[:, :, 0, 0] = 0
    a = (NV - 1) * coin(16, D); a[:, 7, 15] = 0
    ka = 4095 * coin(16); ka[:, 0, 0] = 0; ka[:, 7, 15] = 4095
    th = 4080 * (rng.random((N, 8, 16)) < rng.choice(np.array([0.1, 0.3, 0.6]), (N, 8, 1))).astype(np.int64); th[:, 0, 0] = 0; th[:, 7, 15] = 4080
    return pack(v, a, l, z, c, ka, th)
def setup_inputs_corners(rng):
    v, a, l, z, c, ka, th = parts(rng); h = NV // 2; late = int(rng.integers(0, 7)); last = int(rng.integers(0, 8))
    for r in range(N):
        kinds = rng.permutation(np.array([1, 2, 3, 4, 5, 7])).tolist(); kinds.insert(late, 0); kinds.insert(last, 6)
        for g, kind in enumerate(kinds):
            if kind < 5:
                n = (0, int(rng.choice(np.array([1, 15]))), Q - 1, Q, 16)[kind]
                if kind == 0 or (kind + r) % 2 == 0:
                    d = rng.integers(129, 250, 16); odd = r & 1 if kind == 0 else 1 if kind == 4 else int(rng.integers(0, 2))
                    d[0] -= (int(np.add.reduce(d)) - odd) & 3
                else:
                    d = rng.integers(3, 120, 16)
                p = rng.integers(0, 256 - d); e = int(np.add.reduce(d))
                v[r, g, :, :h] = p[:, None]; v[r, g, :, h:] = (p + d)[:, None]
                l[r, g] = np.where(rng.random((16, B)) < 0.5, rng.integers(0, h, (16, B)), rng.choice(np.array([0, h - 1]), (16, B)))
                a[r, g] = np.where(rng.random((16, D)) < 0.5, rng.integers(h, NV, (16, D)), rng.choice(np.array([h, NV - 1]), (16, D)))
                t = rng.choice(np.array([e - 1, e - 32, e - 33]), 16); o = rng.permutation(16); t[o[:n]] = e
                if kind == 0:
                    t[o[Q - 1:]] = e - 32 * (RO - 1) - rng.integers(0, 2, 17 - Q); c[r, g] = int(rng.integers(0, B))
                th[r, g] = t
            elif kind == 5:
                o = rng.permutation(B)[:M]; c[r, g] = o
                l[r, g][:, o] = 16 * np.arange(M)[None, :] + np.arange(16)[:, None]
                a[r, g] = rng.choice(np.array([0, NV - 1]), (16, D))
            elif kind == 6:
                j = np.arange(NV) & 15; v[r, g] = np.where((j > 0) & (j < 8), 0, np.maximum(v[r, g], 1))
                l[r, g] = 16 * rng.integers(0, M, (16, B)) + rng.integers(1, 8, (16, B))
                a[r, g] = 16 * rng.integers(0, M, (16, D)) + rng.integers(1, 8, (16, D)); a[r, g, 15] = 16 * rng.integers(0, M, D) + rng.integers(8, 16, D)
                x = rng.integers(0, 255, (16, M)); y = (32 - np.add.reduce(x[2:] * (14 * np.arange(2, 16) + 1)[:, None], axis=0)) & 4095
                over = (y > 4080).astype(np.int64); x[2] += over; y = y - 29 * over
                x[1] = np.minimum(y // 15, 255); x[0] = y - 15 * x[1]; z[r, g] = x
                b = (1103 * 32 >> 4) & (B - 1); c[r, g] = b; th[r, g] = 0
                ka[r, g, 15] = ((D - 1 - 37 * 32 - 613 * b) & (D - 1)) + D * int(rng.integers(0, 4096 // D))
            else:
                th[r, g] = 4080 * (r & 1)
    return pack(v, a, l, z, c, ka, th)
def setup_inputs_crowd(rng):
    v, a, l, z, c, ka, th = parts(rng); o = rng.permutation(8).tolist(); q = np.arange(N)
    x = rng.choice(np.array([0, M // 2, M - 1]), N)
    c[:, o[0]] = rng.integers(0, B, (N, 1))
    c[:, o[1]] = rng.integers(0, B, (N, 1)); c[q, o[1], x] = (c[q, o[1], x] + 1) % B
    for g in (o[2], o[3], o[7]):
        z[:, g] = rng.integers(0, 256, (16, 1)); c[:, g] = int(rng.integers(0, B))
    z[q, o[3], :, x] = rng.integers(0, 256, (N, 16))
    two = rng.integers(0, 256, (2, 16)); z[:, o[4]] = two[rng.integers(0, 2, (N, M))].transpose(0, 2, 1); c[:, o[4]] = rng.choice(rng.integers(0, B, 2), (N, M))
    z[:, o[5]] = rng.integers(0, 256, (16, 1))
    z[:, o[6]] = 0; ka[:, o[6]] = 0
    n = int(rng.integers(0, NV)); l[:, o[7]] = n; a[:, o[7]] = (n + int(rng.integers(1, NV))) % NV
    return pack(v, a, l, z, c, ka, th)
def check_inputs(d):
    bad = []
    for k, lo, hi in (("vf", 0, 255), ("ad", 0, NV - 1), ("le", 0, NV - 1), ("z0", 0, 255), ("cb", 0, B - 1), ("ka", 0, 4095), ("th", 0, 4080)):
        x = np.asarray(d[k]); x = x.astype(np.float32) if k in ("vf", "z0") else x
        if not (np.min(x) >= lo and np.max(x) <= hi): bad.append("range of " + k)
        elif k in ("vf", "z0") and np.any(x != np.floor(x)): bad.append("whole numbers in " + k)
    return bad
def hashed(z):
    return np.add.reduce(z * (14 * np.arange(16) + 1)[:, None], axis=2) & 4095
def values(v, x):
    return np.take_along_axis(v, x.reshape(N, 8, 1, 16 * M), 3).reshape(N, 8, 16, 16, M)
def first(x):
    return np.argmax(x[:, :, :, None] == x[:, :, None, :], axis=3) == np.arange(M)
def reference(vf, ad, le, z0, cb, ka, th):
    v = vf.astype(np.float32).astype(np.int32).reshape(N, 8, 16, NV); dirs = ad.astype(np.int64).reshape(N, 8, 16, D); blk = le.astype(np.int64).reshape(N, 8, 16, B)
    z = z0.astype(np.float32).astype(np.int64).reshape(N, 8, 16, M); c = np.stack([gentries(x) for x in cb]).astype(np.int64)
    kap = ka.astype(np.int64).reshape(N, 8, 16, 1); lim = th.astype(np.int64).reshape(N, 8, 16, 1)
    count = np.zeros((N, 8, M), np.int64); u = hashed(z)
    for m in range(1, RO + 1):
        names = np.take_along_axis(blk, c[:, :, None, :], 3)
        a = ((u[:, :, None, :] * kap >> 5) + (37 * u + 613 * c)[:, :, None, :]) & (D - 1)
        n = np.take_along_axis(dirs, a, 3)
        s = values(v, names); y = values(v, n)
        e = np.add.reduce(np.abs(s - y), axis=2)
        ok = e <= lim + 32 * count[:, :, None, :]
        names = np.where(ok, names, n)
        squash = np.add.reduce(ok.astype(np.int64), axis=2) < Q
        hi = np.where(squash[:, :, None, :], np.maximum.reduce(y, axis=3), np.maximum.reduce(np.where(ok[:, :, None], s, -1), axis=3))
        lo = np.where(squash[:, :, None, :], np.minimum.reduce(y, axis=3), np.minimum.reduce(np.where(ok[:, :, None], s, 256), axis=3))
        z = np.abs(z - ((hi.astype(np.int64) + lo) >> 1)); u = hashed(z)
        new = 16 * np.arange(M) + (u & 15)
        np.put_along_axis(v, new[:, :, None, :], z.astype(np.int32), 3)
        r, g, t = np.nonzero(first(c)); blk[r, g, :, c[r, g, t]] = names[r, g, :, t]
        if m == RO: break
        k = np.argmax(e, axis=2)
        col = np.take_along_axis(a, k[:, :, None, :], 2)[:, :, 0]
        r, g, t = np.nonzero(first(col)); dirs[r, g, k[r, g, t], col[r, g, t]] = new[r, g, t]
        count = count + squash; c = (1103 * u >> 4) & (B - 1)
        src = (np.arange(N)[:, None] - np.arange(M) // (M // N) - m) % N
        z = np.take_along_axis(z, src[:, None, None, :], 0); u = np.take_along_axis(u, src[:, None, :], 0)
        c = np.take_along_axis(c, src[:, None, :], 0); count = np.take_along_axis(count, src[:, None, :], 0)
    return {"yv": v.reshape(N, 128, NV).astype(np.float32).astype(BF), "yl": blk.reshape(N, 128, B).astype(np.float32), "yz": z.reshape(N, 128, M).astype(np.float32).astype(BF)}

@@ -1,0 +1,728 @@
+from concourse.bass import DstId, RemoteDMATransfer
+from concourse.mybir import AluOpType as ALU, ActivationFunctionType as AF
+
+BF, F32, F16, I32, U16 = "bfloat16", "float32", "float16", "int32", "uint16"
+SB = {
+    "VF": (4096, BF), "ADi": (1040, I32), "LEi": (1024, I32), "LE": (1040, F32), "z0b": (256, BF),
+    "cW": (16, I32), "kai": (4, I32), "thi": (4, I32),
+    "GA": (4096, F16), "SN0": (4096, BF), "SN1": (4096, BF), "AB": (4096, BF), "WV": (4096, BF),
+    "HI": (4096, BF), "LO": (4096, BF),
+    "snd1": (512, BF), "snd2": (512, BF), "rcv2": (512, BF), "rcv3": (512, BF), "zo": (256, BF),
+    "ones": (128, BF), "BO": (128, BF), "Id": (128, BF), "nI": (128, BF), "n2I": (128, BF), "nI64": (128, BF),
+    "TriI": (128, BF), "MR": (128, BF), "MRt": (128, BF), "M15": (128, BF), "K0": (128, BF), "Ca": (128, BF),
+    "C2k": (128, BF), "Cq": (128, BF), "Z": (144, BF), "Zw": (144, BF),
+    "FS": (2048, BF), "DS": (2048, BF), "GS": (2048, BF), "HS": (2048, BF),
+    "RX": (1024, BF), "RN": (1024, BF), "RB": (256, BF),
+    "pi": (4, I32), "ki": (4, I32), "col": (16, F32), "J16": (16, F32), "RMK": (16, F32), "T16": (16, F32),
+    "M8": (16, F32), "cl16": (8, U16), "kb": (4, I32), "kb2": (4, I32),
+    "ui": (16, I32), "uu": (16, I32), "c1": (16, I32), "b1": (16, I32), "b2": (16, I32), "WF": (32, F16),
+    "c16": (16, U16), "cf": (16, F16), "af": (16, F16), "a16W": (16, U16),
+    "wi": (16, I32), "wl": (16, I32), "w32": (16, F32), "w16": (16, U16), "wp": (16, F16),
+    "fdc": (16, F32), "mxc": (16, F32), "offc": (32, U16), "fda": (16, F32), "mxa": (16, F32), "offa": (32, U16),
+    "xf": (256, F32), "xa": (256, I32), "a32": (256, I32), "a16": (256, U16), "S16": (256, U16), "Sf": (256, F32),
+    "n16": (256, U16), "dn": (256, F32), "nok": (256, BF), "hh": (256, BF), "vv": (256, BF), "p16": (256, U16),
+    "t1": (256, F32), "PM": (256, F32), "ge": (288, BF), "oa": (256, F16), "ohB": (256, BF), "keep": (256, F32),
+    "nw": (256, F32), "y1": (256, F32), "sc": (256, F32), "sa": (256, F32),
+}
+SCRATCH = {k: ("sbuf", [128, v[0]], v[1]) for k, v in SB.items()}
+for _b in range(8):
+    SCRATCH["P%d" % _b] = ("psum", [128, 512], F32)
+DMAS = ["d%d" % i for i in range(16)]
+SEMAPHORES = ["sV", "sA", "sP", "sG", "snt"] + ["arr%d%d" % (m, b) for m in (1, 2) for b in range(8)] + DMAS
+
+MAGIC = 12582912.0
+CO = {"CY": 1.04, "PCY": 0.55, "GC": 1.56, "SCT": 3.8, "LAT": 120.0, "OV": 0.0, "BW": 3000.0}
+_Q4 = [(192, 256), (128, 192), (64, 128), (0, 64)]
+PAR = {
+    "S": {1: "AAAA", 2: "AAAA", 3: "AAAA"},
+    "N": {1: "AAVA", 2: "AAVA", 3: "AAVA"},
+    "R": {1: "AAAA", 2: "AAAA", 3: "AAAA"},
+    "rseg": {1: _Q4, 2: _Q4, 3: _Q4},
+    "tail": {m: [(128, 256), (64, 128), (0, 64)] for m in (1, 2, 3)},
+    "soft": False, "seed": 1, "iters": 50000, "temp": 400.0,
+    "key": {"rc1": -45, "rc0": 2, "S1": 1, "GA1": 1, "N1": 3, "GA0": 4, "mid1": 5, "S0": 6, "N0": 7, "mid0": 8, "R1": 9,
+            "tail1": 10, "R0": 11, "tail0": 12, "arg1": 13, "LE1": 14, "arg0": 15, "LE0": 16, "keep": 17, "AD1": 18, "AD0": 19},
+}
+
+
+def rg(name, lo=0, hi=None, step=1):
+    if hi is None:
+        hi = 512 if name[0] == "P" and name[1:].isdigit() else SB[name][0]
+    return (name, lo, hi, step)
+
+
+def cnt(r):
+    return len(range(r[1], r[2], r[3]))
+
+
+def sub(r, j, st):
+    return (r[0], r[1] + j * r[3], r[2], r[3] * st)
+
+
+def part(r, a, b):
+    return (r[0], r[1] + a * r[3], min(r[2], r[1] + (b - 1) * r[3] + 1), r[3])
+
+
+def isps(r):
+    return r[0][0] == "P" and r[0][1:].isdigit()
+
+
+def two(r):
+    return (not isps(r)) and SB[r[0]][1] in (BF, F16, U16)
+
+
+def build(rank):
+    ops, key = [], [999.0]
+    CY, PCY, GC, SCT, BW = CO["CY"], CO["PCY"], CO["GC"], CO["SCT"], CO["BW"]
+    ENG_S, ENG_N = PAR["S"], PAR["N"]
+
+    def add(eng, kind, args, reads, writes, cost):
+        ops.append((eng, kind, args, [r for r in reads if isinstance(r, tuple)], writes, cost + CO["OV"], None, key[0]))
+
+    def phase(m, name):
+        key[0] = 100.0 * m + PAR["key"][name]
+
+    def either():
+        b, a = ops.pop(), ops.pop()
+        ops.append(a[:3] + (a[3] + b[3],) + a[4:6] + (b[:3] + (b[5],), a[7]))
+
+    def ind(win, off):
+        return ["ind", win, off]
+
+    def rd(x):
+        return [x[1], x[2]] if isinstance(x, list) else [x]
+
+    def vcost(out, ins, tt=False):
+        if isinstance(out, list):
+            return 50 + 16 * cnt(out[2]) * SCT * CY
+        n = cnt(out)
+        if isinstance(ins[0], list):
+            return 50 + n * GC * CY
+        if tt:
+            f = 1 if (isps(ins[0]) or isps(ins[1])) else 2
+        else:
+            f = 0.5 if two(out) and all(two(x) for x in ins) else 1
+        return max(64, n * f) * CY
+
+    def wr(out):
+        return ([out[1]], [out[2]]) if isinstance(out, list) else ([out], [])
+
+    def cp(out, in_):
+        w, r = wr(out)
+        add("V", "cp", (out, in_), rd(in_) + r, w, vcost(out, [in_]))
+
+    def ts(out, in0, s1, op0, s2=None, op1=None):
+        add("V", "ts", (out, in0, s1, s2, op0, op1), rd(in0) + [s1, s2], [out], vcost(out, [in0]))
+
+    def tt(out, in0, in1, op):
+        w, r = wr(out)
+        add("V", "tt", (out, in0, in1, op), rd(in0) + [in1] + r, w, vcost(out, [in0, in1], True))
+
+    def scan(out, d0, d1, op0, op1):
+        add("V", "scan", (out, d0, d1, op0, op1), [d0, d1], [out], vcost(out, [d0, d1]))
+
+    def mset(out, val):
+        add("V", "mset", (out, val), [], [out], vcost(out, [out]))
+
+    def act(out, in_, func, bias=0.0, scale=1.0):
+        n = cnt(out)
+        c = 65 + n * GC * CY if isinstance(in_, list) else max(64, n) * CY + 30
+        add("A", "act", (out, in_, func, bias, scale), rd(in_) + [bias, scale], [out], c)
+
+    def gather(eng, out, src):
+        if eng == "A":
+            act(out, src, AF.Copy)
+            cp(out, src)
+        else:
+            cp(out, src)
+            act(out, src, AF.Copy)
+        either()
+
+    def lin(out, in_, scale, bias):
+        act(out, in_, AF.Identity if isinstance(bias, tuple) or isinstance(scale, tuple) else AF.Copy, bias, scale)
+        ts(out, in_, scale, ALU.mult, bias, ALU.add)
+        either()
+
+    def mm(lst, group=True):
+        reads, writes, c = [], [], 0
+        for o, l, r in lst:
+            reads += [l, r]
+            writes.append(o)
+            c += max(min(64, cnt(l)), cnt(r)) * PCY
+        add("P", "mm", (lst, group), reads, writes, c + 60)
+
+    def iota(out, pat, base, cm):
+        add("G", "iota", (out, pat, base, cm), [], [out], 130 + 2 * cnt(out) * CY)
+
+    def sel(out, in_, pat, op, fill, base, cm):
+        add("G", "sel", (out, in_, pat, op, fill, base, cm), [in_], [out], 170 + 2 * cnt(out) * CY)
+
+    nd = [0]
+
+    def load(out, src, t):
+        add("S", "load", (out, src, DMAS[nd[0]]), [], [out], t)
+        nd[0] += 1
+
+    def store(dst, a, b, in_, t):
+        add("S", "store", (dst, a, b, in_, DMAS[nd[0]]), [in_], [], t)
+        nd[0] += 1
+
+    def c_(j):
+        return rg("col", j, j + 1)
+    KF, WT, DUM, K2, KM4, TH, KAP, CC, K16, THS, KMS = [c_(j) for j in range(11)]
+    E_ = [rg("Z", 15 - j, 143 - j) for j in range(16)]
+    EW = [rg("Zw", 15 - j, 143 - j) for j in range(16)]
+    F_ = [rg("FS", 128 * j, 128 * j + 128) for j in range(16)]
+    D_ = [rg("DS", 128 * j, 128 * j + 128) for j in range(16)]
+    G_ = [rg("GS", 128 * j, 128 * j + 128) for j in range(16)]
+    Id, nI, n2I = rg("Id"), rg("nI"), rg("n2I")
+
+    load(rg("z0b"), "z0", 2000)
+    load(rg("cW"), "cb", 2000)
+    load(rg("kai", 0, 1), "ka", 2100)
+    load(rg("ADi", 0, 1024), "ad", 2100 + 0.5 * BW)
+    load(rg("LEi"), "le", 2100 + BW)
+    load(rg("VF"), "vf", 2100 + 2 * BW)
+    load(rg("thi", 0, 1), "th", 2100 + 2 * BW)
+    mset(rg("ones"), 1.0)
+    iota(rg("pi", 0, 1), [[0, 1]], 0, 1)
+    iota(rg("J16"), [[1, 16]], 0, 0)
+    sel(rg("MRt"), rg("ones"), [[-16, 8], [0, 16]], ALU.is_ge, 0.0, 0, 1)
+    sel(rg("BO"), rg("MRt"), [[16, 8], [0, 16]], ALU.is_ge, 0.0, 15, -1)
+    sel(rg("Id"), rg("ones"), [[-1, 128]], ALU.is_equal, 0.0, 0, 1)
+    ts(rg("ki", 0, 1), rg("pi", 0, 1), 15, ALU.bitwise_and)
+    cp(KF, rg("ki", 0, 1))
+    ts(rg("RMK"), rg("J16"), KF, ALU.is_equal)
+    ts(WT, KF, 14.0, ALU.mult, 1.0, ALU.add)
+    mset(rg("Z"), 0.0)
+    cp(rg("Z", 15, 128, 16), rg("BO", 0, 128, 16))
+    ts(rg("Zw"), rg("Z"), WT, ALU.mult)
+    for j in range(16):
+        lin(F_[j], rg("BO"), rg("RMK", j, j + 1), 0.0)
+    for j in range(16):
+        lin(D_[j], Id, rg("RMK", j, j + 1), 0.0)
+    ts(KAP, rg("kai", 0, 1), 1184.0, ALU.add)
+    ts(rg("kb", 0, 1), rg("kai", 0, 1), 15, ALU.bitwise_and)
+    ts(CC, rg("kb", 0, 1), 2048.0, ALU.mult)
+    cp(TH, rg("thi", 0, 1))
+    act(THS, TH, AF.Copy, -128.0, -256.0)
+    act(KMS, KF, AF.Copy, -896.0, 256.0)
+    act(DUM, KF, AF.Copy, 1024.0)
+    act(K2, KF, AF.Copy, 2048.0)
+    act(KM4, KF, AF.Copy, -4.0)
+    act(K16, KF, AF.Copy, -2048.0, 16.0)
+    act(nI, Id, AF.Copy, 0.0, -1.0)
+    act(n2I, Id, AF.Copy, 0.0, -2.0)
+    act(rg("nI64"), Id, AF.Copy, 0.0, -1.0 / 64)
+    act(rg("M15"), F_[15], AF.Copy, 0.0, -2048.0)
+    act(rg("C2k"), rg("ones"), AF.Copy, 0.0, 2048.0)
+    act(rg("Cq"), rg("ones"), AF.Copy, 0.0, 0.25)
+    sel(rg("TriI"), rg("BO"), [[1, 128]], ALU.is_ge, 0.0, 0, -1)
+    iota(rg("MRt"), [[0, 8], [-1, 16]], 16, 0)
+    ts(rg("MRt"), rg("MRt"), rg("RMK", 15, 16), ALU.mult, -1.0, ALU.add)
+    tt(rg("MR"), rg("MRt"), rg("BO"), ALU.mult)
+    iota(rg("Ca"), [[16, 128]], 0, 0)
+    sel(rg("K0"), rg("ones"), [[0, 8], [1, 16]], ALU.is_equal, 0.0, 0, 0)
+    cp(rg("cl16"), rg("J16", 0, 8))
+    act(rg("T16"), rg("J16"), AF.Identity, K16, 256.0)
+    act(rg("ge", 15, 288, 144), rg("ones", 0, 2), AF.Sigmoid, 0.0, 256.0)
+    ops[-1] = ops[-1][:5] + (ops[-1][5] + 1300, None, 50.0)
+    iota(rg("RX"), [[0, 64], [4096, 16]], 0, 0)
+    iota(rg("RN"), [[0, 64], [-4096, 16]], 256, 0)
+    act(rg("RB"), rg("RN", 0, 256), AF.Copy, 0.0, 2.0 ** 88)
+    sel(rg("HS"), rg("FS"), [[-1, 16], [0, 8], [1, 16]], ALU.is_gt, 0.0, 0, 0)
+    sel(rg("GS"), rg("HS"), [[0, 16], [-1, 128]], ALU.not_equal, -1.0, 0, 1)
+    cp(rg("LE", 0, 1024), rg("LEi"))
+
+    def dedupe(xf, xval, sc, fd, mx, off):
+        mm([(rg("P6", j, 256, 16), G_[j], xf) for j in range(16)], False)
+        scan(sc, rg("RB"), rg("P6", 0, 256), ALU.max, ALU.mult)
+        ts(fd, sub(sc, 15, 16), 0.0, ALU.is_equal, DUM, ALU.mult)
+        tt(mx, fd, xval, ALU.max)
+        cp(rg(off, 0, 32, 2), mx)
+
+    for m in (1, 2, 3):
+        last = m == 3
+        zs, As = {}, {}
+        for h in (1, 0):
+            W = lambda n: rg(n, 8 * h, 8 * h + 8)
+            L = lambda n: rg(n, 128 * h, 128 * h + 128)
+            CH = "P%d" % (2 + h)
+            phase(m, "rc%d" % h)
+            if m == 1:
+                zs[h] = L("z0b")
+            else:
+                zs[h] = rg("rcv%d" % m, 256 * h, 256 * h + 255, 2)
+                As[h] = rg("rcv%d" % m, 256 * h + 1, 256 * h + 256, 2)
+            mm([(rg(CH, 264, 272), EW[j], sub(zs[h], j, 16)) for j in range(16)])
+            cp(W("ui"), rg(CH, 264, 272))
+            ts(W("uu"), W("ui"), 4095, ALU.bitwise_and)
+            ts(rg("WF", 16 * h, 16 * h + 8), W("uu"), -2048.0, ALU.add)
+            if m > 1:
+                ts(W("c1"), W("uu"), 1103.0, ALU.mult)
+                ts(W("cW"), W("c1"), 4, ALU.arith_shift_right, 1023, ALU.bitwise_and)
+            cp(W("c16"), W("cW"))
+            ts(W("cf"), W("cW"), 1.0, ALU.add, 1.0 / 1024, ALU.mult)
+            ts(W("b1"), W("cW"), 613.0, ALU.mult)
+            ts(W("b2"), W("b1"), 1023, ALU.bitwise_and)
+            ts(rg("WF", 16 * h + 8, 16 * h + 16), W("b2"), 32.0, ALU.mult)
+            mm([(rg("P7", 256 * h + j, 256 * h + 256, 16), F_[j], rg("WF", 16 * h, 16 * h + 16)) for j in range(16)], False)
+            lin(L("xf"), rg("P7", 256 * h, 256 * h + 128), KAP, CC)
+            tt(L("xa"), L("xf"), rg("P7", 256 * h + 128, 256 * h + 256), ALU.add)
+            ts(L("a32"), L("xa"), 5, ALU.arith_shift_right, 1023, ALU.bitwise_and)
+            cp(L("a16"), L("a32"))
+            gather("A", L("Sf"), ind(rg("LE", 0, 1024), W("c16")))
+            cp(L("S16"), L("Sf"))
+        for q in (3, 2, 1, 0):
+            h, qq = q // 2, q % 2
+            CH, SN = "P%d" % (2 + h), "SN%d" % h
+            Q = lambda n: rg(n, 64 * q, 64 * q + 64)
+            B = lambda n: rg(n, 1024 * q, 1024 * q + 1024)
+            phase(m, "S%d" % h)
+            gather(ENG_S[m][q], rg(SN, 1024 * qq, 1024 * qq + 1024), ind(rg("VF"), Q("S16")))
+            phase(m, "GA%d" % h)
+            ts(B("GA"), ind(rg("ADi", 0, 1024), Q("a16")), -2048.0, ALU.add)
+            pn = rg(CH, 64 * qq, 64 * qq + 64)
+            mm([(pn, Id, rg("C2k", 0, 64))] + [(pn, D_[k], sub(B("GA"), k, 16)) for k in range(16)])
+            cp(Q("n16"), pn)
+            phase(m, "N%d" % h)
+            gather(ENG_N[m][q], rg(SN, 2048 + 1024 * qq, 3072 + 1024 * qq), ind(rg("VF"), Q("n16")))
+            for x in (0, 1):
+                o = 1024 * qq + 512 * x
+                pd = rg("P%d" % x)
+                mm([(pd, Id, rg(SN, 2048 + o, 2560 + o)), (pd, nI, rg(SN, o, o + 512))])
+                act(rg("AB", 2048 * h + o, 2048 * h + o + 512), pd, AF.Abs)
+            if qq == 0:
+                L = lambda n: rg(n, 128 * h, 128 * h + 128)
+                SD = "P%d" % (4 + h)
+                phase(m, "mid%d" % h)
+                ab = rg("AB", 2048 * h, 2048 * h + 2048)
+                tt(L("dn"), rg(CH, 0, 128), L("Sf"), ALU.subtract)
+                pk = rg("P7", 256 * h, 256 * h + 128)
+                pe = rg(CH, 128, 256)
+                mm([(pe, E_[k], sub(ab, k, 16)) for k in range(16)] + ([(pe, rg("nI64"), As[h])] if m > 1 else []))
+                ts(L("nok"), pe, TH, ALU.is_gt)
+                act(L("nok"), pe, AF.Sigmoid, THS, 256.0)
+                either()
+                mm([(rg(CH, 256, 384), rg("TriI"), L("nok"))])
+                ts(L("hh"), rg(CH, 256, 384), KM4, ALU.is_le)
+                act(L("hh"), rg(CH, 256, 384), AF.Sigmoid, KMS, -256.0)
+                either()
+                mm([(rg(CH, 384, 512), rg("MR"), L("hh"))])
+                tt(L("vv"), rg(CH, 384, 512), L("nok"), ALU.mult)
+                pp = rg(CH, 0, 128)
+                mm([(pp, Id, rg("Ca")), (pp, rg("M15"), L("hh")), (pp, Id, L("vv"))])
+                ts(L("p16"), pp, K2, ALU.add)
+                phase(m, "arg%d" % h)
+                mm([(pk, Id, L("nok"))])
+                tt(L("t1"), L("dn"), pk, ALU.mult)
+                if not last:
+                    mm([(rg(SD, k, 128, 16), sub(ab, k, 16), rg("BO", 0, 128, 16)) for k in range(16)], False)
+                    scan(L("PM"), rg("RX", 0, 128), rg(SD, 0, 128), ALU.min, ALU.max)
+                    g0 = 144 * h + 16
+                    cp(rg("M8", 8 * h, 8 * h + 8), sub(L("PM"), 15, 16))
+                    act(rg("M8", 8 * h, 8 * h + 8), sub(L("PM"), 15, 16), AF.Copy)
+                    either()
+                    tt(rg("ge", g0, g0 + 128), ind(rg("M8", 8 * h, 8 * h + 8), rg("cl16")), L("PM"), ALU.is_equal)
+                    po = rg(SD, 128, 256)
+                    mm([(po, rg("K0"), Id), (po, rg("ge", g0, g0 + 128), Id), (po, rg("ge", g0 - 1, g0 + 127), nI)])
+                    tt(L("oa"), po, L("a32"), ALU.mult)
+                    lin(L("ohB"), po, 4096.0, 0.0)
+                    pa = rg(SD, 256, 384)
+                    mm([(pa, rg("M15"), L("hh"))] + ([(pa, Id, As[h])] if m > 1 else []))
+                    lin(rg("snd%d" % m, 256 * h + 1, 256 * h + 256, 2), pa, 1.0, 2048.0)
+        phase(m, "LE1")
+        dedupe(rg("cf"), rg("cW"), rg("sc"), rg("fdc"), rg("mxc"), "offc")
+        for s in range(15, -1, -1):
+            phase(m, "LE%d" % (s // 8))
+            tt(ind(rg("LE"), rg("offc", 2 * s, 2 * s + 1)), rg("Sf", 16 * s, 16 * s + 16), rg("t1", 16 * s, 16 * s + 16), ALU.add)
+        if last:
+            store("yl", 0, 1024, rg("LE", 0, 1024), 3500)
+        else:
+            phase(m, "keep")
+            pw = rg("P6", 256, 272)
+            mm([(pw, E_[j], sub(rg("oa"), j, 16)) for j in range(16)])
+            cp(rg("a16W"), pw)
+            ts(rg("af"), pw, 1.0, ALU.add, 1.0 / 1024, ALU.mult)
+            tt(rg("keep"), ind(rg("ADi", 0, 1024), rg("a16W")), rg("ohB"), ALU.subtract)
+            dedupe(rg("af"), pw, rg("sa"), rg("fda"), rg("mxa"), "offa")
+        tails = {a: b for a, b in PAR["tail"][m]}
+        for x, (t0, t1) in enumerate(PAR["rseg"][m]):
+            h = t0 // 128
+            CH, SN, SD = "P%d" % (2 + h), "SN%d" % h, "P%d" % (4 + h)
+            B = lambda n: rg(n, 16 * t0, 16 * t1)
+            phase(m, "R%d" % h)
+            gather(PAR["R"][m][x], B("WV"), ind(rg(SN), rg("p16", t0, t1)))
+            scan(B("HI"), rg("RX", 0, 16 * (t1 - t0)), B("WV"), ALU.min, ALU.max)
+            scan(B("LO"), rg("RN", 0, 16 * (t1 - t0)), B("WV"), ALU.max, ALU.min)
+            if t0 in tails:
+                t1 = tails[t0]
+                phase(m, "tail%d" % h)
+                n, o = t1 - t0, t0 % 128
+                W = lambda b: rg(b, t0 // 16, t1 // 16)
+                L = lambda b: rg(b, t0, t1)
+                py = rg(CH, 128 + o, 128 + o + n)
+                mm([(py, n2I, rg("Cq", 0, n)), (py, n2I, part(zs[h], o, o + n)), (py, Id, rg("HI", 16 * t0 + 15, 16 * t1, 16)),
+                    (py, Id, rg("LO", 16 * t0 + 15, 16 * t1, 16))])
+                lin(L("y1"), py, 0.5, MAGIC)
+                zn = L("zo") if last else rg("snd%d" % m, 2 * t0, 2 * t1 - 1, 2)
+                act(zn, L("y1"), AF.Abs, -MAGIC)
+                if not last:
+                    snd, rcv, sem = "snd%d" % m, "rcv%d" % (m + 1), "arr%d%d" % (m, t0 // 32)
+                    bs = [b for b in range(t0 // 32, t1 // 32) if (b + m) % 8]
+                    tok = ("tok", 8 * m + t0 // 32, 8 * m + t0 // 32 + 1, 1)
+                    share = n // 32
+                    add("G", "send", (snd, rcv, bs, m, sem, share), [rg(snd, 2 * t0, 2 * t1)], [tok], 1000)
+                    add("X", "arr", (sem, len(bs), share), [tok], [rg(rcv, 64 * b, 64 * b + 64) for b in bs], 1700 + 250 * share)
+                    for b in range(t0 // 32, t1 // 32):
+                        if (b + m) % 8 == 0:
+                            gather("A", rg(rcv, 64 * b, 64 * b + 64), rg(snd, 64 * b, 64 * b + 64))
+                pu = rg(CH, 256 + o // 16, 256 + (o + n) // 16)
+                mm([(pu, EW[j], sub(zn, j, 16)) for j in range(16)])
+                cp(W("wi"), pu)
+                ts(W("wl"), W("wi"), 15, ALU.bitwise_and)
+                tt(W("wp"), W("wl"), W("T16"), ALU.add)
+                ts(W("w16"), W("wp"), 2048.0 - 16.0 * t0, ALU.add)
+                cp(ind(rg("VF", 16 * t0, 16 * t1), W("w16")), zn)
+                if last:
+                    store("yv", 16 * t0, 16 * t1, rg("VF", 16 * t0, 16 * t1), 2000 + 12 * n)
+                    if o == 0:
+                        store("yz", t0, t0 + 128, rg("zo", t0, t0 + 128), 2200)
+                else:
+                    phase(m, "AD%d" % h)
+                    pb = rg(SD, 384 + o, 384 + o + n)
+                    mm([(pb, nI, rg("C2k", 0, n)), (pb, Id, L("ohB"))] + [(sub(pb, j, 16), F_[j], W("wp")) for j in range(16)])
+                    tt(L("nw"), L("keep"), pb, ALU.max)
+                    for s in range(t1 // 16 - 1, t0 // 16 - 1, -1):
+                        cp(ind(rg("ADi"), rg("offa", 2 * s, 2 * s + 1)), rg("nw", 16 * s, 16 * s + 16))
+    return ops
+
+
+def overlap(a, b):
+    if a[0] != b[0]:
+        return False
+    la = a[1] + (cnt(a) - 1) * a[3]
+    lb = b[1] + (cnt(b) - 1) * b[3]
+    return a[1] <= lb and b[1] <= la
+
+
+def depend(ops):
+    deps, hard, hist = [], [], {}
+    for i, o in enumerate(ops):
+        d, hd = set(), set()
+        for kind, regs in (("r", o[3]), ("w", o[4])):
+            for r in regs:
+                ps = isps(r)
+                for (j, k2, r2) in hist.get(r[0], []):
+                    other = ops[j][0] != o[0] or o[6] or ops[j][6] or o[0] not in "VAP"
+                    if ps and other:
+                        d.add(j)
+                        hd.add(j)
+                    elif (kind == "w" or k2 == "w") and overlap(r, r2):
+                        d.add(j)
+                        if other or kind == "r" or not PAR["soft"]:
+                            hd.add(j)
+        d.discard(i)
+        hd.discard(i)
+        hard.append(hd)
+        for kind, regs in (("r", o[3]), ("w", o[4])):
+            seen = set()
+            for r in regs:
+                if (kind, r) not in seen:
+                    seen.add((kind, r))
+                    hist.setdefault(r[0], []).append((i, kind, r))
+        deps.append(d)
+    anc, red = [], []
+    for i, d in enumerate(deps):
+        a = 0
+        for j in d:
+            a |= anc[j]
+        red.append(sorted(j for j in d if not (a >> j) & 1))
+        for j in d:
+            a |= 1 << j
+        anc.append(0 if ops[i][0] == "X" else a)
+    cov, done, sanc, waits = [], [], [], []
+    for i, d in enumerate(deps):
+        c, sa = 0, 0
+        for j in d - hard[i]:
+            c |= cov[j]
+            sa |= sanc[j] | 1 << j
+        a = c
+        for j in hard[i]:
+            a |= done[j] & ~(1 << j)
+        waits.append(sorted(j for j in hard[i] if not (a >> j) & 1))
+        for j in hard[i]:
+            c |= done[j]
+        if ops[i][0] == "X":
+            c = 0
+        cov.append(c)
+        sanc.append(sa)
+        done.append(c | sa | 1 << i)
+    return red, waits
+
+
+def schedule(ops, deps):
+    n = len(ops)
+    succ = [[] for _ in range(n)]
+    for i in range(n):
+        for j in deps[i]:
+            succ[j].append(i)
+    pr = [0.0] * n
+    for i in range(n - 1, -1, -1):
+        pr[i] = max([pr[k] + 1e-3 for k in succ[i]] + [-ops[i][7] - i * 1e-6])
+    start, fin = place(ops, deps, succ, pr)
+    return sorted(range(n), key=lambda k: (start[k], k)), start, fin
+
+
+def place(ops, deps, succ, pr):
+    n, LAT = len(ops), CO["LAT"]
+    left = [len(d) for d in deps]
+    rdy = {i: 0.0 for i in range(n) if not left[i]}
+    busy = {e: [] for e in "VAPGSX"}
+    fin, start = [0.0] * n, [0.0] * n
+    while rdy:
+        i = max(rdy, key=lambda k: (pr[k], -k))
+        s = rdy.pop(i)
+        e, d = ops[i][0], ops[i][5]
+        if e == "S":
+            s += 60.0 * min(i, 8)
+        elif e != "X":
+            at = 0
+            for a, b in busy[e]:
+                if s + d <= a:
+                    break
+                s = max(s, b)
+                at += 1
+            busy[e].insert(at, (s, s + d))
+        start[i], fin[i] = s, s + d
+        for k in succ[i]:
+            left[k] -= 1
+            if not left[k]:
+                rdy[k] = max(fin[j] + LAT for j in deps[k])
+    return start, fin
+
+
+def replay(order, eng, cost, deps, lat, a=0, old=None):
+    n = len(order)
+    free, lastop = [0.0] * 6, [None] * 6
+    if a:
+        fin, why = list(old[0]), list(old[1])
+        miss = 5
+        for k in range(a - 1, -1, -1):
+            i = order[k]
+            e = eng[i]
+            if e < 5 and lastop[e] is None:
+                lastop[e], free[e] = i, (fin[i] if e < 4 else fin[i] - cost[i] + 60.0)
+                miss -= 1
+                if not miss:
+                    break
+        lastop[4] = None
+    else:
+        fin, why = [0.0] * n, [None] * n
+    for i in order[a:]:
+        e = eng[i]
+        s, w = free[e], lastop[e]
+        if w is not None:
+            w = ~w
+        for j in deps[i]:
+            t = fin[j] + lat
+            if t > s:
+                s, w = t, j
+        f = s + cost[i]
+        fin[i], why[i] = f, w
+        if e < 4:
+            free[e], lastop[e] = f, i
+        elif e == 4:
+            free[4] = s + 60.0
+    return fin, why
+
+
+def improve(ops, deps, waits, order, scen, iters, seed):
+    n = len(ops)
+    EI = {e: k for k, e in enumerate("VAPGSX")}
+    pick = [0] * n
+    flex = [i for i in range(n) if ops[i][6]]
+    st = [seed]
+
+    def rnd():
+        st[0] = (st[0] * 6364136223846793005 + 1442695040888963407) % 18446744073709551616
+        return (st[0] >> 11) / 9007199254740992.0
+
+    def tabs(pick):
+        return ([EI[ops[i][6][0] if pick[i] else ops[i][0]] for i in range(n)],
+                [[so[i][6][3] if pick[i] else so[i][5] for i in range(n)] for so, _l, _w in scen])
+
+    def ev(order, tb, a, olds):
+        res = [replay(order, tb[0], tb[1][k], waits, scen[k][1], a, olds and olds[k]) for k in range(len(scen))]
+        return sum(scen[k][2] * max(r[0]) for k, r in enumerate(res)), res
+    tb = tabs(pick)
+    cur, res = ev(order, tb, 0, None)
+    best = (cur, order, pick)
+    for it in range(iters):
+        temp = PAR["temp"] * (1.0 - it / iters) + 5.0
+        fin, why = res[int(rnd() * len(scen))]
+        arcs, i = [], fin.index(max(fin))
+        while i is not None:
+            w = why[i]
+            if w is not None and w < 0:
+                w = ~w
+                arcs.append((w, i))
+            i = w
+        no, npk = order, pick
+        r = rnd()
+        if r < 0.12 or not arcs:
+            on = [x for a in arcs for x in a if ops[x][6]]
+            f = on[int(rnd() * len(on))] if on and rnd() < 0.7 else flex[int(rnd() * len(flex))]
+            npk = list(pick)
+            npk[f] ^= 1
+            if rnd() < 0.4:
+                a = order.index(f)
+                near = [x for x in order[a + 1:a + 60] if ops[x][6] and tb[0][x] != tb[0][f] and abs(ops[x][5] - ops[f][5]) < 200]
+                if near:
+                    npk[near[int(rnd() * len(near))]] ^= 1
+            ntb, a = tabs(npk), order.index(f)
+        else:
+            ntb = tb
+            k = int(rnd() * len(arcs))
+            u, v = arcs[k]
+            while rnd() < 0.5 and k + 1 < len(arcs) and arcs[k + 1][1] == u:
+                k += 1
+                u = arcs[k][0]
+            a, b = order.index(u), order.index(v)
+            seg = order[a:b + 1]
+            if r < 0.56:
+                need = {v}
+                for x in reversed(seg):
+                    if x in need:
+                        need.update(deps[x])
+                if u in need:
+                    continue
+                seg = [x for x in seg if x in need] + [x for x in seg if x not in need]
+            else:
+                aft = {u}
+                for x in seg:
+                    if any(j in aft for j in deps[x]):
+                        aft.add(x)
+                if v in aft:
+                    continue
+                seg = [x for x in seg if x not in aft] + [x for x in seg if x in aft]
+            no = order[:a] + seg + order[b + 1:]
+        val, nres = ev(no, ntb, a, res)
+        if val <= cur or rnd() < 2.718281828 ** ((cur - val) / temp):
+            cur, pick, res, tb, order = val, npk, nres, ntb, no
+            if it % 8 == 0:
+                f0, c0 = res[0][0], tb[1][0]
+                order = sorted(no, key=lambda x: round(f0[x] - c0[x], 3))
+            if cur < best[0]:
+                best = (cur, order, pick)
+    return best
+
+
+PLAN = {}
+SCEN = [({}, 0.6), ({"GC": 1.3, "SCT": 5.0, "LAT": 200.0, "PCY": 0.7, "OV": 30.0}, 0.4)]
+
+
+def plan():
+    if not PLAN:
+        base, scen = dict(CO), []
+        for sc, w in SCEN:
+            CO.update(sc)
+            scen.append((build(0), CO["LAT"], w))
+            CO.update(base)
+        ops = scen[0][0]
+        every, deps = depend(ops)
+        val, order, pick = improve(ops, every, deps, schedule(ops, every)[0], scen, PAR["iters"], PAR["seed"])
+        ops = [o[6][:3] + o[3:5] + (o[6][3], None, o[7]) if pick[i] else o for i, o in enumerate(ops)]
+        PLAN["p"] = (ops, deps, order, val, pick)
+    return PLAN["p"]
+
+
+def rank_program(g, core, T, topo):
+    rank = T.rank_of(core)
+    if rank is None:
+        return
+    ops, deps, order, _s, _f = plan()
+    Q = {"V": g.vector, "A": g.scalar, "P": g.tensor, "G": g, "S": g.sync}
+    needed = set(j for i, d in enumerate(deps) for j in d if ops[i][0] != "X")
+
+    def ap(x):
+        if isinstance(x, list):
+            return ap(x[1]).indirect(ap(x[2]))
+        if isinstance(x, tuple):
+            return T[x[0]][:, x[1]:x[2]:x[3]] if x[3] != 1 else T[x[0]][:, x[1]:x[2]]
+        return x
+
+    sig, count, waited, total = {}, {}, {}, {}
+    for i in order:
+        e, kind, a = ops[i][:3]
+        if kind in ("load", "store"):
+            sig[i] = (a[-1], 16)
+        elif kind == "arr":
+            src = T.cores[(rank + 1) % len(T.cores)]
+            sig[i] = (a[0], a[1] * (len(topo.engines(src, core)) // a[2]))
+        elif kind != "send" and i in needed:
+            count[e] = count.get(e, 0) + 1
+            sig[i] = ("s" + e, count[e])
+        if i in sig:
+            total[sig[i][0]] = sig[i][1]
+    sent = 0
+    for i in order:
+        e, kind, a = ops[i][:3]
+        if e == "X":
+            continue
+        q = Q[e]
+        want = {}
+        for j in deps[i]:
+            s, v = sig[j]
+            want[s] = max(want.get(s, 0), v)
+        for s, v in want.items():
+            if waited.get((e, s), 0) < v:
+                q.wait_ge(T.sem[s], v)
+                waited[(e, s)] = v
+        if kind == "cp":
+            ins = q.tensor_copy(ap(a[0]), ap(a[1]))
+        elif kind == "ts":
+            if a[5] is None:
+                ins = q.tensor_scalar(ap(a[0]), ap(a[1]), ap(a[2]), None, a[4])
+            else:
+                ins = q.tensor_scalar(ap(a[0]), ap(a[1]), ap(a[2]), ap(a[3]), a[4], a[5])
+        elif kind == "tt":
+            ins = q.tensor_tensor(ap(a[0]), ap(a[1]), ap(a[2]), a[3])
+        elif kind == "scan":
+            ins = q.tensor_tensor_scan(ap(a[0]), ap(a[1]), ap(a[2]), 0.0, a[3], a[4])
+        elif kind == "mset":
+            ins = q.memset(ap(a[0]), a[1])
+        elif kind == "act":
+            ins = q.activation(ap(a[0]), ap(a[1]), a[2], bias=ap(a[3]), scale=ap(a[4]))
+        elif kind == "mm":
+            for k, (o, l, r) in enumerate(a[0]):
+                ins = q.matmul(ap(o), ap(l), ap(r), k == 0 or not a[1], k == len(a[0]) - 1 or not a[1])
+        elif kind == "iota":
+            if SB[a[0][0]][1] == I32:
+                ins = q.iota(ap(a[0]), a[1], a[2], a[3])
+            else:
+                ins = q.iota(ap(a[0]), a[1], a[2], a[3], allow_small_or_imprecise_dtypes=True)
+        elif kind == "sel":
+            ins = q.affine_select(ap(a[0]), ap(a[1]), a[2], a[3], a[4], a[5], a[6])
+        elif kind == "load":
+            ins = q.dma_start(ap(a[0]), T[a[1]][:])
+        elif kind == "store":
+            ins = q.dma_start(T[a[0]][:, a[1]:a[2]], ap(a[3]))
+        elif kind == "send":
+            trs = []
+            for k, b in enumerate(a[2]):
+                dst = T.cores[(rank + b + a[3]) % len(T.cores)]
+                rid, pid = topo.addr(dst)[:2]
+                en = topo.engines(core, dst)
+                w = len(en) // a[5]
+                mask = sum(1 << x for x in en[k * w:(k + 1) * w])
+                trs.append(RemoteDMATransfer(dst_ids=[DstId(rid=rid, pnc=pid)], dma_engine_mask=mask, remote_sem=T.sem[a[4]],
+                                             src=T[a[0]][:, 64 * b:64 * b + 64], dst=T[a[1]][:, 64 * b:64 * b + 64]))
+                sent += w
+            g.remote_dma_fused(trs, local_sem=T.sem.snt)
+            continue
+        if i in sig:
+            ins.then_inc(T.sem[sig[i][0]], 16 if kind in ("load", "store") else 1)
+    total["snt"] = sent
+    for s, v in total.items():
+        g.wait_ge(T.sem[s], v)

@@ -3,52 +3,62 @@ from concourse.mybir import AluOpType as ALU, ActivationFunctionType as AF
 
 BF, F32, F16, I32, U16 = "bfloat16", "float32", "float16", "int32", "uint16"
 SB = {
-    "VF": (4096, BF), "ADi": (1040, I32), "LEi": (1024, I32), "LE": (1040, F32), "z0b": (256, BF),
+    "VF": (8192, BF), "ADi": (1040, I32), "LEi": (1024, I32), "LE": (1040, F32), "z0b": (256, BF),
     "cW": (16, I32), "kai": (4, I32), "thi": (4, I32),
-    "GA": (4096, F16), "SN0": (4096, BF), "SN1": (4096, BF), "AB": (4096, BF), "WV": (4096, BF),
-    "HI": (4096, BF), "LO": (4096, BF),
+    "GA": (4096, F16), "AB": (4096, BF), "WV": (4096, BF), "HI": (4096, BF), "LO": (4096, BF),
     "snd1": (512, BF), "snd2": (512, BF), "rcv2": (512, BF), "rcv3": (512, BF), "zo": (256, BF),
     "ones": (128, BF), "BO": (128, BF), "Id": (128, BF), "nI": (128, BF), "n2I": (128, BF), "nI64": (128, BF),
-    "TriI": (128, BF), "MR": (128, BF), "MRt": (128, BF), "M15": (128, BF), "K0": (128, BF), "Ca": (128, BF),
+    "I32": (128, BF), "nI16": (128, BF), "nI4k": (128, BF), "F32": (128, BF), "MA1": (128, BF), "MA2": (128, BF),
+    "TriI": (128, BF), "MR": (128, BF), "MRt": (128, BF), "MAt": (128, BF), "Ca": (128, BF),
+    "Ck": (128, F16), "MS": (512, BF),
     "C2k": (128, BF), "Cq": (128, BF), "Z": (144, BF), "Zw": (144, BF),
     "FS": (2048, BF), "DS": (2048, BF), "GS": (2048, BF), "HS": (2048, BF),
-    "RX": (1024, BF), "RN": (1024, BF), "RB": (256, BF),
+    "RX": (1024, BF), "RN": (1024, BF), "RB": (256, BF), "RA": (128, BF),
     "pi": (4, I32), "ki": (4, I32), "col": (16, F32), "J16": (16, F32), "RMK": (16, F32), "T16": (16, F32),
-    "M8": (16, F32), "cl16": (8, U16), "kb": (4, I32), "kb2": (4, I32),
+    "kb": (4, I32),
     "ui": (16, I32), "uu": (16, I32), "c1": (16, I32), "b1": (16, I32), "b2": (16, I32), "WF": (32, F16),
     "c16": (16, U16), "cf": (16, F16), "af": (16, F16), "a16W": (16, U16),
-    "wi": (16, I32), "wl": (16, I32), "w32": (16, F32), "w16": (16, U16), "wp": (16, F16),
+    "wi": (16, I32), "wl": (16, I32), "w16": (16, U16), "wp": (16, F16),
     "fdc": (16, F32), "mxc": (16, F32), "offc": (32, U16), "fda": (16, F32), "mxa": (16, F32), "offa": (32, U16),
     "xf": (256, F32), "xa": (256, I32), "a32": (256, I32), "a16": (256, U16), "S16": (256, U16), "Sf": (256, F32),
     "n16": (256, U16), "dn": (256, F32), "nok": (256, BF), "hh": (256, BF), "vv": (256, BF), "p16": (256, U16),
-    "t1": (256, F32), "PM": (256, F32), "ge": (288, BF), "oa": (256, F16), "ohB": (256, BF), "keep": (256, F32),
+    "t1": (256, F32), "PM": (256, F16), "PL": (256, F16), "oa": (256, F16), "noh": (256, BF), "keep": (256, F32),
     "nw": (256, F32), "y1": (256, F32), "sc": (256, F32), "sa": (256, F32),
 }
 SCRATCH = {k: ("sbuf", [128, v[0]], v[1]) for k, v in SB.items()}
 for _b in range(8):
     SCRATCH["P%d" % _b] = ("psum", [128, 512], F32)
-DMAS = ["d%d" % i for i in range(16)]
+DMAS = ["d%d" % i for i in range(24)]
 SEMAPHORES = ["sV", "sA", "sP", "sG", "snt"] + ["arr%d%d" % (m, b) for m in (1, 2) for b in range(8)] + DMAS
 
 MAGIC = 12582912.0
-CO = {"CY": 1.04, "PCY": 0.55, "GC": 1.56, "SCT": 3.8, "LAT": 120.0, "OV": 0.0, "BW": 3000.0}
-_Q4 = [(192, 256), (128, 192), (64, 128), (0, 64)]
+CO = {"CY": 0.88, "PCY": 0.45, "GC": 1.5, "SCT": 3.6, "LAT": 200.0, "OV": 0.0, "BW": 2500.0, "BL": 3000.0, "FX": 1300.0,
+      "SND": 700.0, "ARR": 1500.0}
+_H, _Q = [(128, 256), (0, 128)], [(192, 256), (128, 192), (64, 128), (0, 64)]
+_T = [(128, 256), (64, 128), (0, 64)]
 PAR = {
-    "S": {1: "AAAA", 2: "AAAA", 3: "AAAA"},
-    "N": {1: "AAVA", 2: "AAVA", 3: "AAVA"},
-    "R": {1: "AAAA", 2: "AAAA", 3: "AAAA"},
-    "rseg": {1: _Q4, 2: _Q4, 3: _Q4},
-    "tail": {m: [(128, 256), (64, 128), (0, 64)] for m in (1, 2, 3)},
-    "soft": False, "seed": 1, "iters": 50000, "temp": 400.0,
-    "key": {"rc1": -45, "rc0": 2, "S1": 1, "GA1": 1, "N1": 3, "GA0": 4, "mid1": 5, "S0": 6, "N0": 7, "mid0": 8, "R1": 9,
-            "tail1": 10, "R0": 11, "tail0": 12, "arg1": 13, "LE1": 14, "arg0": 15, "LE0": 16, "keep": 17, "AD1": 18, "AD0": 19},
+    "rc": {1: _H, 2: _H, 3: _H}, "gat": _Q, "mid": _Q, "R": _Q, "tail": _T, "ddc": _H, "dda": [(0, 256)],
+    "abs": 1024, "ttu": True, "even": 0.6,
+    "due": ["G0V:0 G1A:0 S0A:1.4 S1V:1.4 N0V:2.8 N1A:2.8 G2V:4.2 G3A:6.2 S2V:5.6 S3A:7.6 N2V:7 N3A:9 R0A:11 R1A:12.4 R2A:15 R3A:16.4"]
+    + ["S0A:0 S1A:1.4 G1A:2.8 S2A:4.2 N1A:5.6 S3A:9 N3A:10.4 G0V:2.8 G2V:4.2 N0V:5.6 G3V:7 N2V:8.4 R0A:12.8 R1A:14.2 R2A:16.6 R3A:18"] * 2,
+    "step": 26000.0, "wait": 30.0, "lean": 200.0,
+    "seed": 1, "iters": 24000, "temp": 60.0, "tries": 1500, "heat": 30.0, "pull": 2.0,
 }
+PS = {"A": ((3, 0), (2, 0)), "B": ((1, 0), (0, 0)), "u": ((7, 256), (7, 272)), "w": ((1, 272), (0, 272)),
+      "aw": ((6, 288), (6, 304)), "pa": ((7, 0), (7, 128)),
+      "C": ((5, 0), (4, 0)), "D": ((3, 128), (2, 128)), "E": ((3, 256), (2, 256)), "SD": ((5, 384), (4, 384)),
+      "dc": ((6, 0), (6, 128)), "da": ((5, 128), (5, 256))}
 
 
 def rg(name, lo=0, hi=None, step=1):
     if hi is None:
         hi = 512 if name[0] == "P" and name[1:].isdigit() else SB[name][0]
     return (name, lo, hi, step)
+
+
+def ps(name, t0, t1, mul=1, div=1):
+    b, o = PS[name][t0 // 128]
+    return ("P%d" % b, o + (t0 % 128) * mul // div, o + (t0 % 128 + t1 - t0) * mul // div, 1)
 
 
 def cnt(r):
@@ -71,20 +81,16 @@ def two(r):
     return (not isps(r)) and SB[r[0]][1] in (BF, F16, U16)
 
 
-def build(rank):
-    ops, key = [], [999.0]
+def build():
+    ops = []
     CY, PCY, GC, SCT, BW = CO["CY"], CO["PCY"], CO["GC"], CO["SCT"], CO["BW"]
-    ENG_S, ENG_N = PAR["S"], PAR["N"]
 
     def add(eng, kind, args, reads, writes, cost):
-        ops.append((eng, kind, args, [r for r in reads if isinstance(r, tuple)], writes, cost + CO["OV"], None, key[0]))
-
-    def phase(m, name):
-        key[0] = 100.0 * m + PAR["key"][name]
+        ops.append((eng, kind, args, [r for r in reads if isinstance(r, tuple)], writes, cost + CO["OV"], None))
 
     def either():
         b, a = ops.pop(), ops.pop()
-        ops.append(a[:3] + (a[3] + b[3],) + a[4:6] + (b[:3] + (b[5],), a[7]))
+        ops.append(a[:3] + (a[3] + b[3],) + a[4:6] + (b[:3] + (b[5],),))
 
     def ind(win, off):
         return ["ind", win, off]
@@ -126,21 +132,29 @@ def build(rank):
 
     def act(out, in_, func, bias=0.0, scale=1.0):
         n = cnt(out)
-        c = 65 + n * GC * CY if isinstance(in_, list) else max(64, n) * CY + 30
+        c = 65 + n * GC * CY if isinstance(in_, list) else max(64, n) * CY + 20
         add("A", "act", (out, in_, func, bias, scale), rd(in_) + [bias, scale], [out], c)
 
-    def gather(eng, out, src):
-        if eng == "A":
-            act(out, src, AF.Copy)
-            cp(out, src)
+    def lin(out, in_, scale=1.0, bias=0.0):
+        act(out, in_, AF.Identity if isinstance(bias, tuple) or isinstance(scale, tuple) else AF.Copy, bias, scale)
+        if scale == 1.0 and bias == 0.0:
+            cp(out, in_)
+        elif scale == 1.0:
+            ts(out, in_, bias, ALU.add)
+        elif bias == 0.0:
+            ts(out, in_, scale, ALU.mult)
         else:
-            cp(out, src)
-            act(out, src, AF.Copy)
+            ts(out, in_, scale, ALU.mult, bias, ALU.add)
         either()
 
-    def lin(out, in_, scale, bias):
-        act(out, in_, AF.Identity if isinstance(bias, tuple) or isinstance(scale, tuple) else AF.Copy, bias, scale)
-        ts(out, in_, scale, ALU.mult, bias, ALU.add)
+    def relu(out, in_, bias):
+        act(out, in_, AF.Relu, bias)
+        ts(out, in_, bias, ALU.add, 0.0, ALU.max)
+        either()
+
+    def above(out, in_, lim, sgn, slim):
+        act(out, in_, AF.Sigmoid, slim, 256.0 * sgn)
+        ts(out, in_, lim, ALU.is_gt if sgn > 0 else ALU.is_lt)
         either()
 
     def mm(lst, group=True):
@@ -149,7 +163,7 @@ def build(rank):
             reads += [l, r]
             writes.append(o)
             c += max(min(64, cnt(l)), cnt(r)) * PCY
-        add("P", "mm", (lst, group), reads, writes, c + 60)
+        add("P", "mm", (lst, group), reads, writes, c + 50)
 
     def iota(out, pat, base, cm):
         add("G", "iota", (out, pat, base, cm), [], [out], 130 + 2 * cnt(out) * CY)
@@ -159,17 +173,19 @@ def build(rank):
 
     nd = [0]
 
-    def load(out, src, t):
-        add("S", "load", (out, src, DMAS[nd[0]]), [], [out], t)
+    def dma(kind, args, reads, writes, t):
+        add("S", kind, args + (DMAS[nd[0]],), reads, writes, t)
         nd[0] += 1
 
+    def load(out, src, t):
+        dma("load", (out, src, 0, cnt(out)), [], [out], t)
+
     def store(dst, a, b, in_, t):
-        add("S", "store", (dst, a, b, in_, DMAS[nd[0]]), [in_], [], t)
-        nd[0] += 1
+        dma("store", (dst, a, b, in_), [in_], [], t)
 
     def c_(j):
         return rg("col", j, j + 1)
-    KF, WT, DUM, K2, KM4, TH, KAP, CC, K16, THS, KMS = [c_(j) for j in range(11)]
+    KF, WT, DUM, KAP, CC, K16, TH, THS, KM, KMS, TO, TOS = [c_(j) for j in range(12)]
     E_ = [rg("Z", 15 - j, 143 - j) for j in range(16)]
     EW = [rg("Zw", 15 - j, 143 - j) for j in range(16)]
     F_ = [rg("FS", 128 * j, 128 * j + 128) for j in range(16)]
@@ -177,13 +193,14 @@ def build(rank):
     G_ = [rg("GS", 128 * j, 128 * j + 128) for j in range(16)]
     Id, nI, n2I = rg("Id"), rg("nI"), rg("n2I")
 
-    load(rg("z0b"), "z0", 2000)
-    load(rg("cW"), "cb", 2000)
-    load(rg("kai", 0, 1), "ka", 2100)
-    load(rg("ADi", 0, 1024), "ad", 2100 + 0.5 * BW)
-    load(rg("LEi"), "le", 2100 + BW)
-    load(rg("VF"), "vf", 2100 + 2 * BW)
-    load(rg("thi", 0, 1), "th", 2100 + 2 * BW)
+    FX, BL = CO["FX"], CO["BL"]
+    load(rg("z0b"), "z0", FX + 200)
+    load(rg("cW"), "cb", FX + 200)
+    load(rg("kai", 0, 1), "ka", FX + 200)
+    load(rg("ADi", 0, 1024), "ad", FX + 0.5 * BL)
+    load(rg("LEi"), "le", FX + BL)
+    load(rg("VF", 0, 4096), "vf", FX + 2 * BL)
+    load(rg("thi", 0, 1), "th", FX + 2 * BL)
     mset(rg("ones"), 1.0)
     iota(rg("pi", 0, 1), [[0, 1]], 0, 1)
     iota(rg("J16"), [[1, 16]], 0, 0)
@@ -191,178 +208,181 @@ def build(rank):
     sel(rg("BO"), rg("MRt"), [[16, 8], [0, 16]], ALU.is_ge, 0.0, 15, -1)
     sel(rg("Id"), rg("ones"), [[-1, 128]], ALU.is_equal, 0.0, 0, 1)
     ts(rg("ki", 0, 1), rg("pi", 0, 1), 15, ALU.bitwise_and)
-    cp(KF, rg("ki", 0, 1))
+    lin(KF, rg("ki", 0, 1))
     ts(rg("RMK"), rg("J16"), KF, ALU.is_equal)
-    ts(WT, KF, 14.0, ALU.mult, 1.0, ALU.add)
     mset(rg("Z"), 0.0)
-    cp(rg("Z", 15, 128, 16), rg("BO", 0, 128, 16))
-    ts(rg("Zw"), rg("Z"), WT, ALU.mult)
+    lin(rg("Z", 15, 128, 16), rg("BO", 0, 128, 16))
+    mset(rg("Zw"), 0.0)
+    zw = rg("Zw", 15, 128, 16)
+    iota(zw, [[-224, 8]], 1, 14)
+    sel(zw, zw, [[-16, 8]], ALU.is_ge, 0.0, 0, 1)
+    sel(zw, zw, [[16, 8]], ALU.is_ge, 0.0, 15, -1)
     for j in range(16):
-        lin(F_[j], rg("BO"), rg("RMK", j, j + 1), 0.0)
+        lin(F_[j], rg("BO"), rg("RMK", j, j + 1))
     for j in range(16):
-        lin(D_[j], Id, rg("RMK", j, j + 1), 0.0)
-    ts(KAP, rg("kai", 0, 1), 1184.0, ALU.add)
+        lin(D_[j], Id, rg("RMK", j, j + 1))
+    lin(KAP, rg("kai", 0, 1), 1.0, 1184.0)
     ts(rg("kb", 0, 1), rg("kai", 0, 1), 15, ALU.bitwise_and)
-    ts(CC, rg("kb", 0, 1), 2048.0, ALU.mult)
-    cp(TH, rg("thi", 0, 1))
-    act(THS, TH, AF.Copy, -128.0, -256.0)
-    act(KMS, KF, AF.Copy, -896.0, 256.0)
-    act(DUM, KF, AF.Copy, 1024.0)
-    act(K2, KF, AF.Copy, 2048.0)
-    act(KM4, KF, AF.Copy, -4.0)
-    act(K16, KF, AF.Copy, -2048.0, 16.0)
-    act(nI, Id, AF.Copy, 0.0, -1.0)
-    act(n2I, Id, AF.Copy, 0.0, -2.0)
-    act(rg("nI64"), Id, AF.Copy, 0.0, -1.0 / 64)
-    act(rg("M15"), F_[15], AF.Copy, 0.0, -2048.0)
-    act(rg("C2k"), rg("ones"), AF.Copy, 0.0, 2048.0)
-    act(rg("Cq"), rg("ones"), AF.Copy, 0.0, 0.25)
+    lin(CC, rg("kb", 0, 1), 2048.0)
+    lin(TH, rg("thi", 0, 1), 1.0, 0.5)
+    lin(THS, rg("thi", 0, 1), -256.0, -128.0)
+    lin(KM, KF, 1.0, -3.5)
+    lin(KMS, KF, 256.0, -896.0)
+    lin(TO, rg("RMK", 0, 1), -2049.0, 0.5)
+    lin(TOS, rg("RMK", 0, 1), -2049.0 * 256, 128.0)
+    lin(DUM, KF, 1.0, 1024.0)
+    lin(K16, KF, 16.0)
+    for name, x in (("nI", -1.0), ("n2I", -2.0), ("nI64", -1.0 / 64), ("I32", 32.0), ("nI16", -16.0), ("nI4k", -4096.0)):
+        lin(rg(name), Id, x)
+    lin(rg("F32"), F_[15], 32.0)
+    iota(rg("Ca"), [[16, 128]], -2048, 0)
+    lin(rg("Ck"), rg("Ca"), 1.0, KF)
+    for t0, t1 in PAR["mid"]:
+        lin(rg("MS", 2 * t0, 2 * t0 + 128), F_[15], 10240.0 - 16 * t1)
+    lin(rg("C2k"), rg("ones"), 2048.0)
+    lin(rg("Cq"), rg("ones"), 0.25)
     sel(rg("TriI"), rg("BO"), [[1, 128]], ALU.is_ge, 0.0, 0, -1)
     iota(rg("MRt"), [[0, 8], [-1, 16]], 16, 0)
-    ts(rg("MRt"), rg("MRt"), rg("RMK", 15, 16), ALU.mult, -1.0, ALU.add)
+    lin(rg("MRt"), rg("MRt"), rg("RMK", 15, 16), -1.0)
     tt(rg("MR"), rg("MRt"), rg("BO"), ALU.mult)
-    iota(rg("Ca"), [[16, 128]], 0, 0)
-    sel(rg("K0"), rg("ones"), [[0, 8], [1, 16]], ALU.is_equal, 0.0, 0, 0)
-    cp(rg("cl16"), rg("J16", 0, 8))
-    act(rg("T16"), rg("J16"), AF.Identity, K16, 256.0)
-    act(rg("ge", 15, 288, 144), rg("ones", 0, 2), AF.Sigmoid, 0.0, 256.0)
-    ops[-1] = ops[-1][:5] + (ops[-1][5] + 1300, None, 50.0)
+    for t0, t1 in PAR["tail"]:
+        lin(rg("T16", t0 // 16, t1 // 16), rg("J16", 0, (t1 - t0) // 16), 256.0, K16)
+    act(rg("PL", 0, 2), rg("ones", 0, 2), AF.Sigmoid, 0.0, 256.0)
+    ops[-1] = ops[-1][:5] + (ops[-1][5] + 1300, None)
     iota(rg("RX"), [[0, 64], [4096, 16]], 0, 0)
     iota(rg("RN"), [[0, 64], [-4096, 16]], 256, 0)
-    act(rg("RB"), rg("RN", 0, 256), AF.Copy, 0.0, 2.0 ** 88)
+    iota(rg("RA"), [[0, 8], [8192, 16]], -2048, 0)
+    lin(rg("RB"), rg("RN", 0, 256), 2.0 ** 88)
     sel(rg("HS"), rg("FS"), [[-1, 16], [0, 8], [1, 16]], ALU.is_gt, 0.0, 0, 0)
     sel(rg("GS"), rg("HS"), [[0, 16], [-1, 128]], ALU.not_equal, -1.0, 0, 1)
-    cp(rg("LE", 0, 1024), rg("LEi"))
+    lin(rg("MAt"), F_[15], -4096.0)
+    sel(rg("MA1"), rg("MAt"), [[-1, 128]], ALU.not_equal, 4096.0, 0, 1)
+    sel(rg("MA1"), rg("MA1"), [[-512, 8], [-33, 16]], ALU.not_equal, 0.0, 15, 32)
+    sel(rg("MA2"), F_[15], [[-1, 128]], ALU.not_equal, -1.0, 1, 1)
+    sel(rg("MA2"), rg("MA2"), [[-512, 8], [-31, 16]], ALU.not_equal, 0.0, 32, 32)
+    lin(rg("LE", 0, 1024), rg("LEi"))
 
-    def dedupe(xf, xval, sc, fd, mx, off):
-        mm([(rg("P6", j, 256, 16), G_[j], xf) for j in range(16)], False)
-        scan(sc, rg("RB"), rg("P6", 0, 256), ALU.max, ALU.mult)
-        ts(fd, sub(sc, 15, 16), 0.0, ALU.is_equal, DUM, ALU.mult)
-        tt(mx, fd, xval, ALU.max)
-        cp(rg(off, 0, 32, 2), mx)
+    def dedupe(t0, t1, place, xf, xval, sc, fd, mx, off):
+        W = lambda n: rg(n, t0 // 16, t1 // 16)
+        pd = ps(place, t0, t1)
+        mm([(sub(pd, j, 16), G_[j], W(xf)) for j in range(16)], False)
+        scan(rg(sc, t0, t1), rg("RB", 0, t1 - t0), pd, ALU.max, ALU.mult)
+        ts(W(fd), rg(sc, t0 + 15, t1, 16), 0.0, ALU.is_equal, DUM, ALU.mult)
+        if PAR["ttu"]:
+            tt(rg(off, t0 // 8, t1 // 8, 2), W(fd), xval, ALU.max)
+        else:
+            tt(W(mx), W(fd), xval, ALU.max)
+            lin(rg(off, t0 // 8, t1 // 8, 2), W(mx))
 
     for m in (1, 2, 3):
         last = m == 3
-        zs, As = {}, {}
-        for h in (1, 0):
-            W = lambda n: rg(n, 8 * h, 8 * h + 8)
-            L = lambda n: rg(n, 128 * h, 128 * h + 128)
-            CH = "P%d" % (2 + h)
-            phase(m, "rc%d" % h)
-            if m == 1:
-                zs[h] = L("z0b")
-            else:
-                zs[h] = rg("rcv%d" % m, 256 * h, 256 * h + 255, 2)
-                As[h] = rg("rcv%d" % m, 256 * h + 1, 256 * h + 256, 2)
-            mm([(rg(CH, 264, 272), EW[j], sub(zs[h], j, 16)) for j in range(16)])
-            cp(W("ui"), rg(CH, 264, 272))
+        zs = lambda a, b: rg("z0b", a, b) if m == 1 else rg("rcv%d" % m, 2 * a, 2 * b - 1, 2)
+        As = lambda a, b: rg("rcv%d" % m, 2 * a + 1, 2 * b, 2)
+        hh = lambda a, b: rg("snd1", 2 * a + 1, 2 * b, 2) if m == 1 else rg("hh", a, b)
+        for t0, t1 in PAR["rc"][m]:
+            n = t1 - t0
+            W = lambda b: rg(b, t0 // 16, t1 // 16)
+            L = lambda b: rg(b, t0, t1)
+            wu, wb = rg("WF", t0 // 8, (t0 + t1) // 16), rg("WF", (t0 + t1) // 16, t1 // 8)
+            pu = ps("u", t0, t1, 1, 16)
+            mm([(pu, EW[j], sub(zs(t0, t1), j, 16)) for j in range(16)])
+            lin(W("ui"), pu)
             ts(W("uu"), W("ui"), 4095, ALU.bitwise_and)
-            ts(rg("WF", 16 * h, 16 * h + 8), W("uu"), -2048.0, ALU.add)
+            lin(wu, W("uu"), 1.0, -2048.0)
             if m > 1:
-                ts(W("c1"), W("uu"), 1103.0, ALU.mult)
+                lin(W("c1"), W("uu"), 1103.0)
                 ts(W("cW"), W("c1"), 4, ALU.arith_shift_right, 1023, ALU.bitwise_and)
-            cp(W("c16"), W("cW"))
-            ts(W("cf"), W("cW"), 1.0, ALU.add, 1.0 / 1024, ALU.mult)
-            ts(W("b1"), W("cW"), 613.0, ALU.mult)
+            lin(W("c16"), W("cW"))
+            lin(W("cf"), W("cW"), 1.0 / 1024, 1.0 / 1024)
+            lin(W("b1"), W("cW"), 613.0)
             ts(W("b2"), W("b1"), 1023, ALU.bitwise_and)
-            ts(rg("WF", 16 * h + 8, 16 * h + 16), W("b2"), 32.0, ALU.mult)
-            mm([(rg("P7", 256 * h + j, 256 * h + 256, 16), F_[j], rg("WF", 16 * h, 16 * h + 16)) for j in range(16)], False)
-            lin(L("xf"), rg("P7", 256 * h, 256 * h + 128), KAP, CC)
-            tt(L("xa"), L("xf"), rg("P7", 256 * h + 128, 256 * h + 256), ALU.add)
+            lin(wb, W("b2"), 32.0)
+            pb = ps("D", t0, t1, 2)
+            mm([(sub(pb, j, 16), F_[j], rg("WF", t0 // 8, t1 // 8)) for j in range(16)], False)
+            lin(L("xf"), part(pb, 0, n), KAP, CC)
+            tt(L("xa"), L("xf"), part(pb, n, 2 * n), ALU.add)
             ts(L("a32"), L("xa"), 5, ALU.arith_shift_right, 1023, ALU.bitwise_and)
-            cp(L("a16"), L("a32"))
-            gather("A", L("Sf"), ind(rg("LE", 0, 1024), W("c16")))
-            cp(L("S16"), L("Sf"))
-        for q in (3, 2, 1, 0):
-            h, qq = q // 2, q % 2
-            CH, SN = "P%d" % (2 + h), "SN%d" % h
-            Q = lambda n: rg(n, 64 * q, 64 * q + 64)
-            B = lambda n: rg(n, 1024 * q, 1024 * q + 1024)
-            phase(m, "S%d" % h)
-            gather(ENG_S[m][q], rg(SN, 1024 * qq, 1024 * qq + 1024), ind(rg("VF"), Q("S16")))
-            phase(m, "GA%d" % h)
-            ts(B("GA"), ind(rg("ADi", 0, 1024), Q("a16")), -2048.0, ALU.add)
-            pn = rg(CH, 64 * qq, 64 * qq + 64)
-            mm([(pn, Id, rg("C2k", 0, 64))] + [(pn, D_[k], sub(B("GA"), k, 16)) for k in range(16)])
-            cp(Q("n16"), pn)
-            phase(m, "N%d" % h)
-            gather(ENG_N[m][q], rg(SN, 2048 + 1024 * qq, 3072 + 1024 * qq), ind(rg("VF"), Q("n16")))
-            for x in (0, 1):
-                o = 1024 * qq + 512 * x
-                pd = rg("P%d" % x)
-                mm([(pd, Id, rg(SN, 2048 + o, 2560 + o)), (pd, nI, rg(SN, o, o + 512))])
-                act(rg("AB", 2048 * h + o, 2048 * h + o + 512), pd, AF.Abs)
-            if qq == 0:
-                L = lambda n: rg(n, 128 * h, 128 * h + 128)
-                SD = "P%d" % (4 + h)
-                phase(m, "mid%d" % h)
-                ab = rg("AB", 2048 * h, 2048 * h + 2048)
-                tt(L("dn"), rg(CH, 0, 128), L("Sf"), ALU.subtract)
-                pk = rg("P7", 256 * h, 256 * h + 128)
-                pe = rg(CH, 128, 256)
-                mm([(pe, E_[k], sub(ab, k, 16)) for k in range(16)] + ([(pe, rg("nI64"), As[h])] if m > 1 else []))
-                ts(L("nok"), pe, TH, ALU.is_gt)
-                act(L("nok"), pe, AF.Sigmoid, THS, 256.0)
-                either()
-                mm([(rg(CH, 256, 384), rg("TriI"), L("nok"))])
-                ts(L("hh"), rg(CH, 256, 384), KM4, ALU.is_le)
-                act(L("hh"), rg(CH, 256, 384), AF.Sigmoid, KMS, -256.0)
-                either()
-                mm([(rg(CH, 384, 512), rg("MR"), L("hh"))])
-                tt(L("vv"), rg(CH, 384, 512), L("nok"), ALU.mult)
-                pp = rg(CH, 0, 128)
-                mm([(pp, Id, rg("Ca")), (pp, rg("M15"), L("hh")), (pp, Id, L("vv"))])
-                ts(L("p16"), pp, K2, ALU.add)
-                phase(m, "arg%d" % h)
-                mm([(pk, Id, L("nok"))])
-                tt(L("t1"), L("dn"), pk, ALU.mult)
-                if not last:
-                    mm([(rg(SD, k, 128, 16), sub(ab, k, 16), rg("BO", 0, 128, 16)) for k in range(16)], False)
-                    scan(L("PM"), rg("RX", 0, 128), rg(SD, 0, 128), ALU.min, ALU.max)
-                    g0 = 144 * h + 16
-                    cp(rg("M8", 8 * h, 8 * h + 8), sub(L("PM"), 15, 16))
-                    act(rg("M8", 8 * h, 8 * h + 8), sub(L("PM"), 15, 16), AF.Copy)
-                    either()
-                    tt(rg("ge", g0, g0 + 128), ind(rg("M8", 8 * h, 8 * h + 8), rg("cl16")), L("PM"), ALU.is_equal)
-                    po = rg(SD, 128, 256)
-                    mm([(po, rg("K0"), Id), (po, rg("ge", g0, g0 + 128), Id), (po, rg("ge", g0 - 1, g0 + 127), nI)])
-                    tt(L("oa"), po, L("a32"), ALU.mult)
-                    lin(L("ohB"), po, 4096.0, 0.0)
-                    pa = rg(SD, 256, 384)
-                    mm([(pa, rg("M15"), L("hh"))] + ([(pa, Id, As[h])] if m > 1 else []))
-                    lin(rg("snd%d" % m, 256 * h + 1, 256 * h + 256, 2), pa, 1.0, 2048.0)
-        phase(m, "LE1")
-        dedupe(rg("cf"), rg("cW"), rg("sc"), rg("fdc"), rg("mxc"), "offc")
-        for s in range(15, -1, -1):
-            phase(m, "LE%d" % (s // 8))
-            tt(ind(rg("LE"), rg("offc", 2 * s, 2 * s + 1)), rg("Sf", 16 * s, 16 * s + 16), rg("t1", 16 * s, 16 * s + 16), ALU.add)
+            lin(L("a16"), L("a32"))
+            for out in ("S16", "Sf"):
+                lin(L(out), ind(rg("LEi" if m == 1 else "LE", 0, 1024), W("c16")))
+        nb = 0
+        for t0, t1 in PAR["mid"]:
+            n = t1 - t0
+            for q0, q1 in PAR["gat"]:
+                if not t0 <= q0 < t1:
+                    continue
+                Q = lambda b: rg(b, q0, q1)
+                B = lambda b: rg(b, 16 * q0, 16 * q1)
+                sv = rg("VF", 8192 - 16 * (t1 + t0 - q0), 8192 - 16 * (t1 + t0 - q1))
+                lin(sv, ind(rg("VF", 0, 4096), Q("S16")))
+                lin(B("GA"), ind(rg("ADi", 0, 1024), Q("a16")), 1.0, -2048.0)
+                pn = ps("C", q0, q1)
+                mm([(pn, Id, rg("C2k", 0, q1 - q0))] + [(pn, D_[k], sub(B("GA"), k, 16)) for k in range(16)])
+                lin(Q("n16"), pn)
+                tt(B("AB"), ind(rg("VF", 0, 4096), Q("n16")), sv, ALU.subtract)
+                for o in range(16 * q0, 16 * q1, PAR["abs"]):
+                    act(rg("AB", o, min(o + PAR["abs"], 16 * q1)), rg("AB", o, min(o + PAR["abs"], 16 * q1)), AF.Abs)
+            L = lambda b: rg(b, t0, t1)
+            ab = rg("AB", 16 * t0, 16 * t1)
+            pa, pb, pc = ps("A", t0, t1), ps("B", t0, t1), ps("C", t0, t1)
+            tt(L("dn"), pc, L("Sf"), ALU.subtract)
+            mm([(pa, E_[k], sub(ab, k, 16)) for k in range(16)] + [(pa, rg("nI64"), rg("C2k", 0, n))] * (m == 2)
+               + ([(pa, rg("F32"), As(t0, t1))] if m > 1 else []))
+            above(L("nok"), pa, TH, 1, THS)
+            mm([(pb, rg("TriI"), L("nok"))])
+            above(hh(t0, t1), pb, KM, -1, KMS)
+            mm([(pa, rg("MR"), hh(t0, t1)), (pa, rg("I32"), L("nok"))])
+            relu(L("vv"), pa, -16.0)
+            mm([(pb, Id, rg("Ck", 0, n)), (pb, rg("MS", 2 * t0, 2 * t0 + 128), hh(t0, t1)), (pb, rg("nI16"), L("nok")), (pb, Id, L("vv"))])
+            tt(L("p16"), pb, L("n16"), ALU.max)
+            mm([(pc, Id, L("nok"))])
+            tt(L("t1"), L("dn"), pc, ALU.mult)
+            if m == 2:
+                pq = ps("pa", t0, t1)
+                mm([(pq, Id, hh(t0, t1)), (pq, Id, As(t0, t1))])
+                lin(rg("snd2", 2 * t0 + 1, 2 * t1, 2), pq, 1.0, -2.0)
+            if not last and t0 % 128 == 0:
+                L = lambda b: rg(b, t0, t0 + 128)
+                ab = rg("AB", 16 * t0, 16 * t0 + 2048)
+                sd, pd, pe = ps("SD", t0, t0 + 128), ps("D", t0, t0 + 128), ps("E", t0, t0 + 128)
+                mm([(sd, nI, rg("C2k"))] + [(sub(sd, k, 16), sub(ab, k, 16), rg("BO", 0, 128, 16)) for k in range(16)])
+                scan(L("PM"), rg("RA"), sd, ALU.min, ALU.max)
+                mm([(pd, L("PM"), Id)])
+                lin(L("PL"), pd)
+                mm([(pe, rg("MA1"), L("PL")), (pe, rg("MA2"), L("PL"))])
+                above(L("noh"), pe, TO, -1, TOS)
+                mm([(sd, Id, rg("ones")), (sd, nI, L("noh"))])
+                tt(L("oa"), sd, L("a32"), ALU.mult)
+        for t0, t1 in PAR["ddc"]:
+            dedupe(t0, t1, "dc", "cf", rg("cW", t0 // 16, t1 // 16), "sc", "fdc", "mxc", "offc")
+            for s in range(t1 // 16 - 1, t0 // 16 - 1, -1):
+                tt(ind(rg("LE"), rg("offc", 2 * s, 2 * s + 1)), rg("Sf", 16 * s, 16 * s + 16), rg("t1", 16 * s, 16 * s + 16), ALU.add)
         if last:
-            store("yl", 0, 1024, rg("LE", 0, 1024), 3500)
+            store("yl", 0, 1024, rg("LE", 0, 1024), FX + BW)
         else:
-            phase(m, "keep")
-            pw = rg("P6", 256, 272)
-            mm([(pw, E_[j], sub(rg("oa"), j, 16)) for j in range(16)])
-            cp(rg("a16W"), pw)
-            ts(rg("af"), pw, 1.0, ALU.add, 1.0 / 1024, ALU.mult)
-            tt(rg("keep"), ind(rg("ADi", 0, 1024), rg("a16W")), rg("ohB"), ALU.subtract)
-            dedupe(rg("af"), pw, rg("sa"), rg("fda"), rg("mxa"), "offa")
-        tails = {a: b for a, b in PAR["tail"][m]}
-        for x, (t0, t1) in enumerate(PAR["rseg"][m]):
-            h = t0 // 128
-            CH, SN, SD = "P%d" % (2 + h), "SN%d" % h, "P%d" % (4 + h)
-            B = lambda n: rg(n, 16 * t0, 16 * t1)
-            phase(m, "R%d" % h)
-            gather(PAR["R"][m][x], B("WV"), ind(rg(SN), rg("p16", t0, t1)))
+            for t0, t1 in PAR["dda"]:
+                W = lambda b: rg(b, t0 // 16, t1 // 16)
+                L = lambda b: rg(b, t0, t1)
+                pw = ps("aw", t0, t1, 1, 16)
+                mm([(pw, E_[j], sub(L("oa"), j, 16)) for j in range(16)])
+                lin(W("a16W"), pw)
+                lin(W("af"), pw, 1.0 / 1024, 1.0 / 1024)
+                tt(L("keep"), ind(rg("ADi", 0, 1024), W("a16W")), L("noh"), ALU.mult)
+                dedupe(t0, t1, "da", "af", pw, "sa", "fda", "mxa", "offa")
+        tails, late = {a: b for a, b in PAR["tail"]}, []
+        for t0, t1 in PAR["R"]:
+            m0, m1 = [x for x in PAR["mid"] if x[0] <= t0 < x[1]][0]
+            B = lambda b: rg(b, 16 * t0, 16 * t1)
+            lin(B("WV"), ind(rg("VF", 0, 8192 - 16 * m0), rg("p16", t0, t1)))
             scan(B("HI"), rg("RX", 0, 16 * (t1 - t0)), B("WV"), ALU.min, ALU.max)
             scan(B("LO"), rg("RN", 0, 16 * (t1 - t0)), B("WV"), ALU.max, ALU.min)
             if t0 in tails:
                 t1 = tails[t0]
-                phase(m, "tail%d" % h)
-                n, o = t1 - t0, t0 % 128
+                n = t1 - t0
                 W = lambda b: rg(b, t0 // 16, t1 // 16)
                 L = lambda b: rg(b, t0, t1)
-                py = rg(CH, 128 + o, 128 + o + n)
-                mm([(py, n2I, rg("Cq", 0, n)), (py, n2I, part(zs[h], o, o + n)), (py, Id, rg("HI", 16 * t0 + 15, 16 * t1, 16)),
+                py = ps("A", t0, t1)
+                mm([(py, n2I, rg("Cq", 0, n)), (py, n2I, zs(t0, t1)), (py, Id, rg("HI", 16 * t0 + 15, 16 * t1, 16)),
                     (py, Id, rg("LO", 16 * t0 + 15, 16 * t1, 16))])
                 lin(L("y1"), py, 0.5, MAGIC)
                 zn = L("zo") if last else rg("snd%d" % m, 2 * t0, 2 * t1 - 1, 2)
@@ -372,151 +392,88 @@ def build(rank):
                     bs = [b for b in range(t0 // 32, t1 // 32) if (b + m) % 8]
                     tok = ("tok", 8 * m + t0 // 32, 8 * m + t0 // 32 + 1, 1)
                     share = n // 32
-                    add("G", "send", (snd, rcv, bs, m, sem, share), [rg(snd, 2 * t0, 2 * t1)], [tok], 1000)
-                    add("X", "arr", (sem, len(bs), share), [tok], [rg(rcv, 64 * b, 64 * b + 64) for b in bs], 1700 + 250 * share)
+                    if bs:
+                        add("G", "send", (snd, rcv, bs, m, sem, share), [rg(snd, 2 * t0, 2 * t1)], [tok], CO["SND"])
+                        add("X", "arr", (sem, len(bs), share), [tok], [rg(rcv, 64 * b, 64 * b + 64) for b in bs], CO["ARR"] + 250 * share)
                     for b in range(t0 // 32, t1 // 32):
                         if (b + m) % 8 == 0:
-                            gather("A", rg(rcv, 64 * b, 64 * b + 64), rg(snd, 64 * b, 64 * b + 64))
-                pu = rg(CH, 256 + o // 16, 256 + (o + n) // 16)
+                            dma("lcp", (rg(rcv, 64 * b, 64 * b + 64), rg(snd, 64 * b, 64 * b + 64)), [rg(snd, 64 * b, 64 * b + 64)],
+                                [rg(rcv, 64 * b, 64 * b + 64)], 2000)
+                pu = ps("w", t0, t1, 1, 16)
                 mm([(pu, EW[j], sub(zn, j, 16)) for j in range(16)])
-                cp(W("wi"), pu)
+                lin(W("wi"), pu)
                 ts(W("wl"), W("wi"), 15, ALU.bitwise_and)
-                tt(W("wp"), W("wl"), W("T16"), ALU.add)
-                ts(W("w16"), W("wp"), 2048.0 - 16.0 * t0, ALU.add)
-                cp(ind(rg("VF", 16 * t0, 16 * t1), W("w16")), zn)
-                if last:
-                    store("yv", 16 * t0, 16 * t1, rg("VF", 16 * t0, 16 * t1), 2000 + 12 * n)
-                    if o == 0:
-                        store("yz", t0, t0 + 128, rg("zo", t0, t0 + 128), 2200)
-                else:
-                    phase(m, "AD%d" % h)
-                    pb = rg(SD, 384 + o, 384 + o + n)
-                    mm([(pb, nI, rg("C2k", 0, n)), (pb, Id, L("ohB"))] + [(sub(pb, j, 16), F_[j], W("wp")) for j in range(16)])
+                tt(W("w16"), W("wl"), W("T16"), ALU.add)
+                if not last:
+                    lin(W("wp"), W("w16"), 1.0, 16.0 * t0 - 2048.0)
+                late.append((t0, t1, zn))
+                if last and t0 % 128 == 0:
+                    store("yz", t0, t0 + 128, rg("zo", t0, t0 + 128), FX + 300)
+                if not last:
+                    pb = ps("B", t0, t1)
+                    mm([(pb, Id, rg("C2k", 0, n)), (pb, rg("nI4k"), L("noh"))] + [(sub(pb, j, 16), F_[j], W("wp")) for j in range(16)])
                     tt(L("nw"), L("keep"), pb, ALU.max)
                     for s in range(t1 // 16 - 1, t0 // 16 - 1, -1):
                         cp(ind(rg("ADi"), rg("offa", 2 * s, 2 * s + 1)), rg("nw", 16 * s, 16 * s + 16))
+        for t0, t1, zn in late:
+            vf = rg("VF", 16 * t0, 16 * t1)
+            cp(ind(vf, rg("w16", t0 // 16, t1 // 16)), zn)
+            if last:
+                store("yv", 16 * t0, 16 * t1, vf, FX + BW * (t1 - t0) / 128)
     return ops
 
 
 def overlap(a, b):
-    if a[0] != b[0]:
-        return False
     la = a[1] + (cnt(a) - 1) * a[3]
     lb = b[1] + (cnt(b) - 1) * b[3]
     return a[1] <= lb and b[1] <= la
 
 
 def depend(ops):
-    deps, hard, hist = [], [], {}
+    hist, anc, red = {}, [], []
     for i, o in enumerate(ops):
-        d, hd = set(), set()
-        for kind, regs in (("r", o[3]), ("w", o[4])):
-            for r in regs:
-                ps = isps(r)
+        d = set()
+        for kind, regs in ((0, o[3]), (1, o[4])):
+            for r in set(regs):
                 for (j, k2, r2) in hist.get(r[0], []):
-                    other = ops[j][0] != o[0] or o[6] or ops[j][6] or o[0] not in "VAP"
-                    if ps and other:
+                    if (kind or k2) and overlap(r, r2):
                         d.add(j)
-                        hd.add(j)
-                    elif (kind == "w" or k2 == "w") and overlap(r, r2):
-                        d.add(j)
-                        if other or kind == "r" or not PAR["soft"]:
-                            hd.add(j)
-        d.discard(i)
-        hd.discard(i)
-        hard.append(hd)
-        for kind, regs in (("r", o[3]), ("w", o[4])):
-            seen = set()
-            for r in regs:
-                if (kind, r) not in seen:
-                    seen.add((kind, r))
-                    hist.setdefault(r[0], []).append((i, kind, r))
-        deps.append(d)
-    anc, red = [], []
-    for i, d in enumerate(deps):
+        for kind, regs in ((0, o[3]), (1, o[4])):
+            for r in set(regs):
+                hist.setdefault(r[0], []).append((i, kind, r))
         a = 0
         for j in d:
             a |= anc[j]
         red.append(sorted(j for j in d if not (a >> j) & 1))
         for j in d:
             a |= 1 << j
-        anc.append(0 if ops[i][0] == "X" else a)
-    cov, done, sanc, waits = [], [], [], []
-    for i, d in enumerate(deps):
-        c, sa = 0, 0
-        for j in d - hard[i]:
-            c |= cov[j]
-            sa |= sanc[j] | 1 << j
-        a = c
-        for j in hard[i]:
-            a |= done[j] & ~(1 << j)
-        waits.append(sorted(j for j in hard[i] if not (a >> j) & 1))
-        for j in hard[i]:
-            c |= done[j]
-        if ops[i][0] == "X":
-            c = 0
-        cov.append(c)
-        sanc.append(sa)
-        done.append(c | sa | 1 << i)
-    return red, waits
+        anc.append(0 if o[0] == "X" else a)
+    return red
 
 
-def schedule(ops, deps):
-    n = len(ops)
-    succ = [[] for _ in range(n)]
-    for i in range(n):
-        for j in deps[i]:
-            succ[j].append(i)
-    pr = [0.0] * n
-    for i in range(n - 1, -1, -1):
-        pr[i] = max([pr[k] + 1e-3 for k in succ[i]] + [-ops[i][7] - i * 1e-6])
-    start, fin = place(ops, deps, succ, pr)
-    return sorted(range(n), key=lambda k: (start[k], k)), start, fin
+EI = {e: k for k, e in enumerate("VAPGSX")}
 
 
-def place(ops, deps, succ, pr):
-    n, LAT = len(ops), CO["LAT"]
-    left = [len(d) for d in deps]
-    rdy = {i: 0.0 for i in range(n) if not left[i]}
-    busy = {e: [] for e in "VAPGSX"}
-    fin, start = [0.0] * n, [0.0] * n
-    while rdy:
-        i = max(rdy, key=lambda k: (pr[k], -k))
-        s = rdy.pop(i)
-        e, d = ops[i][0], ops[i][5]
-        if e == "S":
-            s += 60.0 * min(i, 8)
-        elif e != "X":
-            at = 0
-            for a, b in busy[e]:
-                if s + d <= a:
-                    break
-                s = max(s, b)
-                at += 1
-            busy[e].insert(at, (s, s + d))
-        start[i], fin[i] = s, s + d
-        for k in succ[i]:
-            left[k] -= 1
-            if not left[k]:
-                rdy[k] = max(fin[j] + LAT for j in deps[k])
-    return start, fin
-
-
-def replay(order, eng, cost, deps, lat, a=0, old=None):
+def replay(order, eng, cost, deps, banks, lat, a=0, old=None):
     n = len(order)
     free, lastop = [0.0] * 6, [None] * 6
+    b1, b2 = [None] * 8, [None] * 8
     if a:
         fin, why = list(old[0]), list(old[1])
-        miss = 5
-        for k in range(a - 1, -1, -1):
-            i = order[k]
+        for i in order[:a]:
             e = eng[i]
-            if e < 5 and lastop[e] is None:
-                lastop[e], free[e] = i, (fin[i] if e < 4 else fin[i] - cost[i] + 60.0)
-                miss -= 1
-                if not miss:
-                    break
-        lastop[4] = None
+            lastop[e] = i
+            for b in banks[i]:
+                j = b1[b]
+                if j is not None and eng[j] != e:
+                    b2[b] = j
+                b1[b] = i
+        for e in range(4):
+            if lastop[e] is not None:
+                free[e] = fin[lastop[e]]
+        if lastop[4] is not None:
+            free[4] = fin[lastop[4]] - cost[lastop[4]] + 60.0
+        lastop[4] = lastop[5] = None
     else:
         fin, why = [0.0] * n, [None] * n
     for i in order[a:]:
@@ -528,6 +485,17 @@ def replay(order, eng, cost, deps, lat, a=0, old=None):
             t = fin[j] + lat
             if t > s:
                 s, w = t, j
+        for b in banks[i]:
+            j = b1[b]
+            if j is not None and eng[j] != e:
+                b2[b] = j
+            else:
+                j = b2[b]
+            b1[b] = i
+            if j is not None:
+                t = fin[j] + lat
+                if t > s:
+                    s, w = t, ~j
         f = s + cost[i]
         fin[i], why[i] = f, w
         if e < 4:
@@ -537,23 +505,66 @@ def replay(order, eng, cost, deps, lat, a=0, old=None):
     return fin, why
 
 
-def improve(ops, deps, waits, order, scen, iters, seed):
-    n = len(ops)
-    EI = {e: k for k, e in enumerate("VAPGSX")}
-    pick = [0] * n
-    flex = [i for i in range(n) if ops[i][6]]
-    st = [seed]
+def listed(deps, succ, banks, opt, dl, lat, wait, lean):
+    n = len(deps)
+    left = [len(d) for d in deps]
+    at = [0.0] * n
+    rdy = [i for i in range(n) if not left[i]]
+    free, bf = [0.0] * 6, [[0.0] * 3 for _ in range(8)]
+    order, pick, end = [], [0] * n, 0.0
+    while rdy:
+        cands, s0, e0 = [], 1e18, 0
+        for i in rdy:
+            bv = 1e18
+            for e, c, k in opt[i]:
+                s = at[i]
+                if free[e] > s:
+                    s = free[e]
+                for b in banks[i]:
+                    x = bf[b]
+                    for e2 in range(3):
+                        if e2 != e and x[e2] > s:
+                            s = x[e2]
+                v = s + c + (lean if e == 0 else 0.0)
+                if v < bv:
+                    best, bv = (s, e, i, k, c), v
+            cands.append(best)
+            if best[0] < s0:
+                s0, e0 = best[:2]
+        bk = 1e18
+        for x in cands:
+            if x[1] == e0 and dl[x[2]] + wait * (x[0] - s0) < bk:
+                bk, bx = dl[x[2]] + wait * (x[0] - s0), x
+        s, e, i, k, c = bx
+        rdy.remove(i)
+        order.append(i)
+        pick[i], f = k, s + c
+        if f > end:
+            end = f
+        if e < 4:
+            free[e] = f
+        elif e == 4:
+            free[e] = s + 60.0
+        for b in banks[i]:
+            bf[b][e] = f + lat
+        for j in succ[i]:
+            if f + lat > at[j]:
+                at[j] = f + lat
+            left[j] -= 1
+            if not left[j]:
+                rdy.append(j)
+    return end, order, pick
 
-    def rnd():
-        st[0] = (st[0] * 6364136223846793005 + 1442695040888963407) % 18446744073709551616
-        return (st[0] >> 11) / 9007199254740992.0
+
+def improve(ops, deps, banks, order, pick, scen, iters, rnd):
+    n = len(ops)
 
     def tabs(pick):
         return ([EI[ops[i][6][0] if pick[i] else ops[i][0]] for i in range(n)],
                 [[so[i][6][3] if pick[i] else so[i][5] for i in range(n)] for so, _l, _w in scen])
 
     def ev(order, tb, a, olds):
-        res = [replay(order, tb[0], tb[1][k], waits, scen[k][1], a, olds and olds[k]) for k in range(len(scen))]
+        res = [replay(order, tb[0], tb[1][k], deps, banks, scen[k][1], a, olds and olds[k]) for k in range(len(scen))]
         return sum(scen[k][2] * max(r[0]) for k, r in enumerate(res)), res
     tb = tabs(pick)
     cur, res = ev(order, tb, 0, None)
@@ -570,17 +581,25 @@ def improve(ops, deps, waits, order, scen, iters, seed):
             i = w
         no, npk = order, pick
         r = rnd()
-        if r < 0.12 or not arcs:
+        if r < 0.2 or not arcs:
             on = [x for a in arcs for x in a if ops[x][6]]
-            f = on[int(rnd() * len(on))] if on and rnd() < 0.7 else flex[int(rnd() * len(flex))]
+            if not on:
+                continue
+            f = on[int(rnd() * len(on))]
             npk = list(pick)
             npk[f] ^= 1
+            a = order.index(f)
+            ch = [f]
             if rnd() < 0.4:
-                a = order.index(f)
-                near = [x for x in order[a + 1:a + 60] if ops[x][6] and tb[0][x] != tb[0][f] and abs(ops[x][5] - ops[f][5]) < 200]
+                near = [x for x in order[a + 1:a + 40] if ops[x][6] and tb[0][x] != tb[0][f] and abs(ops[x][5] - ops[f][5]) < 200]
                 if near:
-                    npk[near[int(rnd() * len(near))]] ^= 1
-            ntb, a = tabs(npk), order.index(f)
+                    ch.append(near[int(rnd() * len(near))])
+                    npk[ch[1]] ^= 1
+            ntb = (list(tb[0]), [list(c) for c in tb[1]])
+            for x in ch:
+                ntb[0][x] = 1 - ntb[0][x]
+                for k, c in enumerate(ntb[1]):
+                    c[x] = scen[k][0][x][6][3] if npk[x] else scen[k][0][x][5]
         else:
             ntb = tb
             k = int(rnd() * len(arcs))
@@ -590,7 +609,7 @@ def improve(ops, deps, waits, order, scen, iters, seed):
                 u = arcs[k][0]
             a, b = order.index(u), order.index(v)
             seg = order[a:b + 1]
-            if r < 0.56:
+            if r < 0.6:
                 need = {v}
                 for x in reversed(seg):
                     if x in need:
@@ -618,8 +637,132 @@ def improve(ops, deps, waits, order, scen, iters, seed):
     return best
 
 
+def place(seq, a, old, deps, banks, eng, cost, lat):
+    st = list(old)
+    lo, hi = [[] for _ in range(4)], [[] for _ in range(4)]
+    bk = [[] for _ in range(8)]
+    for i in seq[:a]:
+        e = eng[i]
+        if e < 4:
+            lo[e].append(st[i])
+            hi[e].append(st[i] + cost[i])
+            for b in banks[i]:
+                bk[b].append((st[i], st[i] + cost[i], e))
+    for i in seq[a:]:
+        t, e, c = 0.0, eng[i], cost[i]
+        for j in deps[i]:
+            x = st[j] + cost[j] + lat
+            if x > t:
+                t = x
+        if e < 4:
+            L, H = lo[e], hi[e]
+            k = len(L)
+            while k and H[k - 1] > t:
+                k -= 1
+            moved = True
+            while moved:
+                moved = False
+                while k < len(L) and L[k] < t + c:
+                    if H[k] > t:
+                        t = H[k]
+                    k += 1
+                for b in banks[i]:
+                    B = bk[b]
+                    q = len(B) - 1
+                    while q >= 0 and B[q][0] + 1500.0 > t:
+                        x, y, e2 = B[q]
+                        if e2 != e and x < t + c + lat and y + lat > t:
+                            t, moved = y + lat, True
+                            break
+                        q -= 1
+            L.insert(k, t)
+            H.insert(k, t + c)
+            for b in banks[i]:
+                B = bk[b]
+                q = len(B)
+                while q and B[q - 1][0] > t:
+                    q -= 1
+                B.insert(q, (t, t + c, e))
+        st[i] = t
+    return st
+
+
+def refine(ops, slow, deps, banks, order, pick, iters, rnd):
+    n, lat = len(ops), CO["LAT"]
+    pick = list(pick)
+    eng = [EI[o[6][0] if pick[i] else o[0]] for i, o in enumerate(ops)]
+    cost = [o[6][3] if pick[i] else o[5] for i, o in enumerate(ops)]
+    flex = [i for i in range(n) if ops[i][6]]
+    big = [i for i in flex if ops[i][5] > 600]
+
+    cost2 = [o[6][3] if pick[i] else o[5] for i, o in enumerate(slow)]
+
+    def value(st):
+        fin = [st[i] + cost[i] for i in range(n)]
+        sq = sorted(range(n), key=lambda i: (st[i], i))
+        fin2 = replay(sq, eng, cost2, deps, banks, lat)[0]
+        end = max(fin) + PAR["even"] * max(fin2)
+        return end + PAR["pull"] * (sum(fin) + PAR["even"] * sum(fin2)) / n, end, sq
+
+    def flip(xs):
+        for x in xs:
+            pick[x] ^= 1
+            eng[x] = 1 - eng[x]
+            cost2[x] = slow[x][6][3] if pick[x] else slow[x][5]
+            cost[x] = ops[x][6][3] if pick[x] else ops[x][5]
+    st = place(order, 0, [0.0] * n, deps, banks, eng, cost, lat)
+    cur, end, seq = value(st)
+    best = (end, seq, list(pick))
+    for it in range(iters):
+        temp = PAR["heat"] * (1.0 - it / iters) + 3.0
+        r, ch = rnd(), []
+        if r < 0.25:
+            pool = big if rnd() < 0.3 else flex
+            ch = [pool[int(rnd() * len(pool))]]
+            if rnd() < 0.5:
+                i = ch[0]
+                near = [j for j in flex if eng[j] != eng[i] and abs(st[j] - st[i]) < 2000 and abs(cost[j] - cost[i]) < 300]
+                if near:
+                    ch.append(near[int(rnd() * len(near))])
+            flip(ch)
+            ns, a = seq, min(seq.index(x) for x in ch)
+        else:
+            i, d = int(rnd() * n), 3000.0 * abs(rnd() + rnd() - 1.0)
+            pr = list(st)
+            if r < 0.65:
+                stack, seen = [i], {i}
+                while stack:
+                    x = stack.pop()
+                    pr[x] -= d
+                    for j in deps[x]:
+                        if j not in seen and st[j] > st[i] - 2500.0:
+                            seen.add(j)
+                            stack.append(j)
+            else:
+                pr[i] += d
+            for x in range(n):
+                for j in deps[x]:
+                    if pr[j] >= pr[x]:
+                        pr[x] = pr[j] + 1e-3
+            ns = sorted(range(n), key=lambda i: pr[i])
+            a = 0
+            while a < n and ns[a] == seq[a]:
+                a += 1
+            if a == n:
+                continue
+        s2 = place(ns, a, st, deps, banks, eng, cost, lat)
+        v, end, sq = value(s2)
+        if v <= cur or rnd() < 2.718281828 ** ((cur - v) / temp):
+            cur, st, seq = v, s2, sq
+            if end < best[0]:
+                best = (end, seq, list(pick))
+        else:
+            flip(ch)
+    return best
+
+
 PLAN = {}
-SCEN = [({}, 0.6), ({"GC": 1.3, "SCT": 5.0, "LAT": 200.0, "PCY": 0.7, "OV": 30.0}, 0.4)]
+SCEN = [({}, 0.6), ({"CY": 1.2, "PCY": 0.6, "GC": 2.0, "SCT": 5.3}, 0.4)]
 
 
 def plan():
@@ -627,13 +770,66 @@ def plan():
         base, scen = dict(CO), []
         for sc, w in SCEN:
             CO.update(sc)
-            scen.append((build(0), CO["LAT"], w))
+            scen.append((build(), CO["LAT"], w))
             CO.update(base)
         ops = scen[0][0]
-        every, deps = depend(ops)
-        val, order, pick = improve(ops, every, deps, schedule(ops, every)[0], scen, PAR["iters"], PAR["seed"])
-        ops = [o[6][:3] + o[3:5] + (o[6][3], None, o[7]) if pick[i] else o for i, o in enumerate(ops)]
-        PLAN["p"] = (ops, deps, order, val, pick)
+        n = len(ops)
+        deps = depend(ops)
+        banks = [sorted(set(int(r[0][1:]) for r in o[3] + o[4] if isps(r))) for o in ops]
+        succ = [[] for _ in range(n)]
+        for i in range(n):
+            for j in deps[i]:
+                succ[j].append(i)
+        st = [PAR["seed"]]
+
+        def rnd():
+            st[0] = (st[0] * 6364136223846793005 + 1442695040888963407) % 18446744073709551616
+            return (st[0] >> 11) / 9007199254740992.0
+        big, seen = {}, {}
+        for i, o in enumerate(ops):
+            if o[0] in "VA" and isinstance(o[2][1], list) and o[4][0][0] in ("VF", "AB", "GA", "WV"):
+                nm = {"S16": "S", "a16": "G", "n16": "N", "p16": "R"}[o[2][1][2][0]]
+                per = len(PAR["R" if nm == "R" else "gat"])
+                seen[nm] = seen.get(nm, -1) + 1
+                big[i] = (seen[nm] // per, nm + str(seen[nm] % per))
+        due = {(m, w[:2]): (1000.0 * float(w[4:]), EI[w[2]]) for m in range(3) for w in PAR["due"][m].split()}
+        for m, k in sorted(big.values()):
+            if (m, k) not in due:
+                t, e = due[(m, k[0] + str(int(k[1]) - 1))]
+                due[(m, k)] = (t + 1000.0, e)
+        keys = sorted(set(k[1] for k in big.values()))
+        both = [[(EI[o[0]], o[5], 0)] + ([(EI[o[6][0]], o[6][3], 1)] if o[6] else []) for o in ops]
+
+        def ev(due):
+            dl, opt = [0.0] * n, list(both)
+            for i in range(n - 1, -1, -1):
+                if i in big:
+                    dl[i] = big[i][0] * PAR["step"] + due[big[i]][0]
+                    opt[i] = [x for x in both[i] if x[0] == due[big[i]][1]] or both[i]
+                else:
+                    dl[i] = min([dl[j] for j in succ[i]] + [3 * PAR["step"] + 3000.0]) - ops[i][5] - CO["LAT"]
+            end, order, pick = listed(deps, succ, banks, opt, dl, CO["LAT"], PAR["wait"], PAR["lean"])
+            eng = [both[i][pick[i]][0] for i in range(n)]
+            cost2 = [o[6][3] if pick[i] else o[5] for i, o in enumerate(scen[1][0])]
+            return end + PAR["even"] * max(replay(order, eng, cost2, deps, banks, CO["LAT"])[0]), order, pick
+        cur = best = ev(due)
+        PLAN["due"] = due
+        for it in range(PAR["tries"]):
+            nd = dict(due)
+            for _ in range(1 + int(3 * rnd())):
+                k, d, flip = keys[int(rnd() * len(keys))], 5000.0 * (rnd() + rnd() - 1.0), rnd() < 0.35
+                for m in (range(3) if rnd() < 0.3 else [int(3 * rnd())]):
+                    t, e = nd[(m, k)]
+                    nd[(m, k)] = (t, 1 - e) if flip else (t + d, e)
+            v = ev(nd)
+            if v[0] <= cur[0] + 300.0 * rnd():
+                cur, due = v, nd
+                if v[0] < best[0]:
+                    best = v
+                    PLAN["due"] = due
+        val, order, pick = refine(ops, scen[1][0], deps, banks, best[1], best[2], PAR["iters"], rnd)
+        ops = [o[6][:3] + o[3:5] + (o[6][3], None) if pick[i] else o for i, o in enumerate(ops)]
+        PLAN["p"] = (ops, deps, banks, order, val, pick, best[0])
     return PLAN["p"]
 
 
@@ -641,9 +837,8 @@ def rank_program(g, core, T, topo):
     rank = T.rank_of(core)
     if rank is None:
         return
-    ops, deps, order, _s, _f = plan()
+    ops, deps, banks, order = plan()[:4]
     Q = {"V": g.vector, "A": g.scalar, "P": g.tensor, "G": g, "S": g.sync}
-    needed = set(j for i, d in enumerate(deps) for j in d if ops[i][0] != "X")
 
     def ap(x):
         if isinstance(x, list):
@@ -652,15 +847,37 @@ def rank_program(g, core, T, topo):
             return T[x[0]][:, x[1]:x[2]:x[3]] if x[3] != 1 else T[x[0]][:, x[1]:x[2]]
         return x
 
-    sig, count, waited, total = {}, {}, {}, {}
+    pos = {i: k for k, i in enumerate(order)}
+    known, done, waits, user = {e: 0 for e in Q}, {}, {}, [{} for _ in range(8)]
+    ran = {e: 0 for e in Q}
+    for i in order:
+        e = ops[i][0]
+        if e == "X":
+            done[i] = 1 << i
+            continue
+        need = set(deps[i])
+        for b in banks[i]:
+            need.update(j for e2, j in user[b].items() if e2 != e)
+            user[b][e] = i
+        waits[i] = []
+        for j in sorted(need, key=lambda x: -pos[x]):
+            if not (known[e] >> j) & 1:
+                waits[i].append(j)
+                known[e] |= done[j]
+        if e == "S" or ops[i][1] == "send":
+            done[i] = known[e] | 1 << i
+        else:
+            ran[e] |= known[e] | 1 << i
+            done[i] = ran[e]
+    sig, count, total = {}, {}, {}
     for i in order:
         e, kind, a = ops[i][:3]
-        if kind in ("load", "store"):
+        if e == "S":
             sig[i] = (a[-1], 16)
         elif kind == "arr":
             src = T.cores[(rank + 1) % len(T.cores)]
             sig[i] = (a[0], a[1] * (len(topo.engines(src, core)) // a[2]))
-        elif kind != "send" and i in needed:
+        elif kind != "send":
             count[e] = count.get(e, 0) + 1
             sig[i] = ("s" + e, count[e])
         if i in sig:
@@ -671,14 +888,8 @@ def rank_program(g, core, T, topo):
         if e == "X":
             continue
         q = Q[e]
-        want = {}
-        for j in deps[i]:
-            s, v = sig[j]
-            want[s] = max(want.get(s, 0), v)
-        for s, v in want.items():
-            if waited.get((e, s), 0) < v:
-                q.wait_ge(T.sem[s], v)
-                waited[(e, s)] = v
+        for j in waits[i]:
+            q.wait_ge(T.sem[sig[j][0]], sig[j][1])
         if kind == "cp":
             ins = q.tensor_copy(ap(a[0]), ap(a[1]))
         elif kind == "ts":
@@ -708,6 +919,8 @@ def rank_program(g, core, T, topo):
             ins = q.dma_start(ap(a[0]), T[a[1]][:])
         elif kind == "store":
             ins = q.dma_start(T[a[0]][:, a[1]:a[2]], ap(a[3]))
+        elif kind == "lcp":
+            ins = q.dma_start(ap(a[0]), ap(a[1]))
         elif kind == "send":
             trs = []
             for k, b in enumerate(a[2]):
@@ -721,8 +934,7 @@ def rank_program(g, core, T, topo):
                 sent += w
             g.remote_dma_fused(trs, local_sem=T.sem.snt)
             continue
-        if i in sig:
-            ins.then_inc(T.sem[sig[i][0]], 16 if kind in ("load", "store") else 1)
+        ins.then_inc(T.sem[sig[i][0]], 16 if e == "S" else 1)
     total["snt"] = sent
     for s, v in total.items():
         g.wait_ge(T.sem[s], v)

from concourse.bass import DstId, RemoteDMATransfer
from concourse.mybir import AluOpType as ALU, ActivationFunctionType as AF

BF, F32, F16, I32, U16 = "bfloat16", "float32", "float16", "int32", "uint16"
SB = {
    "VF": (8192, BF), "ADi": (1040, I32), "LEi": (1024, I32), "LE": (1040, F32), "z0b": (256, BF),
    "cW": (16, I32), "kai": (4, I32), "thi": (4, I32),
    "GA": (4096, F16), "AB": (4096, BF), "WV": (4096, BF), "HI": (4096, BF), "LO": (4096, BF),
    "snd1": (512, BF), "snd2": (512, BF), "rcv2": (512, BF), "rcv3": (512, BF), "zo": (256, BF),
    "ones": (128, BF), "BO": (128, BF), "Id": (128, BF), "nI": (128, BF), "n2I": (128, BF), "nI64": (128, BF),
    "I32": (128, BF), "nI16": (128, BF), "nI4k": (128, BF), "F32": (128, BF), "MA1": (128, BF), "MA2": (128, BF),
    "TriI": (128, BF), "MR": (128, BF), "MRt": (128, BF), "MAt": (128, BF), "Ca": (128, BF),
    "Ck": (128, F16), "MS": (512, BF),
    "C2k": (128, BF), "Cq": (128, BF), "Z": (144, BF), "Zw": (144, BF),
    "FS": (2048, BF), "DS": (2048, BF), "GS": (2048, BF), "HS": (2048, BF),
    "RX": (1024, BF), "RN": (1024, BF), "RB": (256, BF), "RA": (128, BF),
    "pi": (4, I32), "ki": (4, I32), "col": (16, F32), "J16": (16, F32), "RMK": (16, F32), "T16": (16, F32),
    "kb": (4, I32),
    "ui": (16, I32), "uu": (16, I32), "c1": (16, I32), "b1": (16, I32), "b2": (16, I32), "WF": (32, F16),
    "c16": (16, U16), "cf": (16, F16), "af": (16, F16), "a16W": (16, U16),
    "wi": (16, I32), "wl": (16, I32), "w16": (16, U16), "wp": (16, F16),
    "fdc": (16, F32), "mxc": (16, F32), "offc": (32, U16), "fda": (16, F32), "mxa": (16, F32), "offa": (32, U16),
    "xf": (256, F32), "xa": (256, I32), "a32": (256, I32), "a16": (256, U16), "S16": (256, U16), "Sf": (256, F32),
    "n16": (256, U16), "dn": (256, F32), "nok": (256, BF), "hh": (256, BF), "vv": (256, BF), "p16": (256, U16),
    "t1": (256, F32), "PM": (256, F16), "PL": (256, F16), "oa": (256, F16), "noh": (256, BF), "keep": (256, F32),
    "nw": (256, F32), "y1": (256, F32), "sc": (256, F32), "sa": (256, F32),
}
SCRATCH = {k: ("sbuf", [128, v[0]], v[1]) for k, v in SB.items()}
for _b in range(8):
    SCRATCH["P%d" % _b] = ("psum", [128, 512], F32)
DMAS = ["d%d" % i for i in range(24)]
SEMAPHORES = ["sV", "sA", "sP", "sG", "snt"] + ["arr%d%d" % (m, b) for m in (1, 2) for b in range(8)] + DMAS

MAGIC = 12582912.0
CO = {"CY": 0.88, "PCY": 0.45, "GC": 1.5, "SCT": 3.6, "LAT": 200.0, "OV": 0.0, "BW": 2500.0, "BL": 3000.0, "FX": 1300.0,
      "SND": 700.0, "ARR": 1500.0}
_H, _Q = [(128, 256), (0, 128)], [(192, 256), (128, 192), (64, 128), (0, 64)]
_T = [(128, 256), (64, 128), (0, 64)]
PAR = {
    "rc": {1: _H, 2: _H, 3: _H}, "gat": _Q, "mid": _Q, "R": _Q, "tail": _T, "ddc": _H, "dda": [(0, 256)],
    "abs": 1024, "ttu": True, "even": 0.6,
    "due": ["G0V:0 G1A:0 S0A:1.4 S1V:1.4 N0V:2.8 N1A:2.8 G2V:4.2 G3A:6.2 S2V:5.6 S3A:7.6 N2V:7 N3A:9 R0A:11 R1A:12.4 R2A:15 R3A:16.4"]
    + ["S0A:0 S1A:1.4 G1A:2.8 S2A:4.2 N1A:5.6 S3A:9 N3A:10.4 G0V:2.8 G2V:4.2 N0V:5.6 G3V:7 N2V:8.4 R0A:12.8 R1A:14.2 R2A:16.6 R3A:18"] * 2,
    "step": 26000.0, "wait": 30.0, "lean": 200.0,
    "seed": 1, "iters": 24000, "temp": 60.0, "tries": 1500, "heat": 30.0, "pull": 2.0,
}
PS = {"A": ((3, 0), (2, 0)), "B": ((1, 0), (0, 0)), "u": ((7, 256), (7, 272)), "w": ((1, 272), (0, 272)),
      "aw": ((6, 288), (6, 304)), "pa": ((7, 0), (7, 128)),
      "C": ((5, 0), (4, 0)), "D": ((3, 128), (2, 128)), "E": ((3, 256), (2, 256)), "SD": ((5, 384), (4, 384)),
      "dc": ((6, 0), (6, 128)), "da": ((5, 128), (5, 256))}


def rg(name, lo=0, hi=None, step=1):
    if hi is None:
        hi = 512 if name[0] == "P" and name[1:].isdigit() else SB[name][0]
    return (name, lo, hi, step)


def ps(name, t0, t1, mul=1, div=1):
    b, o = PS[name][t0 // 128]
    return ("P%d" % b, o + (t0 % 128) * mul // div, o + (t0 % 128 + t1 - t0) * mul // div, 1)


def cnt(r):
    return len(range(r[1], r[2], r[3]))


def sub(r, j, st):
    return (r[0], r[1] + j * r[3], r[2], r[3] * st)


def part(r, a, b):
    return (r[0], r[1] + a * r[3], min(r[2], r[1] + (b - 1) * r[3] + 1), r[3])


def isps(r):
    return r[0][0] == "P" and r[0][1:].isdigit()


def two(r):
    return (not isps(r)) and SB[r[0]][1] in (BF, F16, U16)


def build():
    ops = []
    CY, PCY, GC, SCT, BW = CO["CY"], CO["PCY"], CO["GC"], CO["SCT"], CO["BW"]

    def add(eng, kind, args, reads, writes, cost):
        ops.append((eng, kind, args, [r for r in reads if isinstance(r, tuple)], writes, cost + CO["OV"], None))

    def either():
        b, a = ops.pop(), ops.pop()
        ops.append(a[:3] + (a[3] + b[3],) + a[4:6] + (b[:3] + (b[5],),))

    def ind(win, off):
        return ["ind", win, off]

    def rd(x):
        return [x[1], x[2]] if isinstance(x, list) else [x]

    def vcost(out, ins, tt=False):
        if isinstance(out, list):
            return 50 + 16 * cnt(out[2]) * SCT * CY
        n = cnt(out)
        if isinstance(ins[0], list):
            return 50 + n * GC * CY
        if tt:
            f = 1 if (isps(ins[0]) or isps(ins[1])) else 2
        else:
            f = 0.5 if two(out) and all(two(x) for x in ins) else 1
        return max(64, n * f) * CY

    def wr(out):
        return ([out[1]], [out[2]]) if isinstance(out, list) else ([out], [])

    def cp(out, in_):
        w, r = wr(out)
        add("V", "cp", (out, in_), rd(in_) + r, w, vcost(out, [in_]))

    def ts(out, in0, s1, op0, s2=None, op1=None):
        add("V", "ts", (out, in0, s1, s2, op0, op1), rd(in0) + [s1, s2], [out], vcost(out, [in0]))

    def tt(out, in0, in1, op):
        w, r = wr(out)
        add("V", "tt", (out, in0, in1, op), rd(in0) + [in1] + r, w, vcost(out, [in0, in1], True))

    def scan(out, d0, d1, op0, op1):
        add("V", "scan", (out, d0, d1, op0, op1), [d0, d1], [out], vcost(out, [d0, d1]))

    def mset(out, val):
        add("V", "mset", (out, val), [], [out], vcost(out, [out]))

    def act(out, in_, func, bias=0.0, scale=1.0):
        n = cnt(out)
        c = 65 + n * GC * CY if isinstance(in_, list) else max(64, n) * CY + 20
        add("A", "act", (out, in_, func, bias, scale), rd(in_) + [bias, scale], [out], c)

    def lin(out, in_, scale=1.0, bias=0.0):
        act(out, in_, AF.Identity if isinstance(bias, tuple) or isinstance(scale, tuple) else AF.Copy, bias, scale)
        if scale == 1.0 and bias == 0.0:
            cp(out, in_)
        elif scale == 1.0:
            ts(out, in_, bias, ALU.add)
        elif bias == 0.0:
            ts(out, in_, scale, ALU.mult)
        else:
            ts(out, in_, scale, ALU.mult, bias, ALU.add)
        either()

    def relu(out, in_, bias):
        act(out, in_, AF.Relu, bias)
        ts(out, in_, bias, ALU.add, 0.0, ALU.max)
        either()

    def above(out, in_, lim, sgn, slim):
        act(out, in_, AF.Sigmoid, slim, 256.0 * sgn)
        ts(out, in_, lim, ALU.is_gt if sgn > 0 else ALU.is_lt)
        either()

    def mm(lst, group=True):
        reads, writes, c = [], [], 0
        for o, l, r in lst:
            reads += [l, r]
            writes.append(o)
            c += max(min(64, cnt(l)), cnt(r)) * PCY
        add("P", "mm", (lst, group), reads, writes, c + 50)

    def iota(out, pat, base, cm):
        add("G", "iota", (out, pat, base, cm), [], [out], 130 + 2 * cnt(out) * CY)

    def sel(out, in_, pat, op, fill, base, cm):
        add("G", "sel", (out, in_, pat, op, fill, base, cm), [in_], [out], 170 + 2 * cnt(out) * CY)

    nd = [0]

    def dma(kind, args, reads, writes, t):
        add("S", kind, args + (DMAS[nd[0]],), reads, writes, t)
        nd[0] += 1

    def load(out, src, t):
        dma("load", (out, src, 0, cnt(out)), [], [out], t)

    def store(dst, a, b, in_, t):
        dma("store", (dst, a, b, in_), [in_], [], t)

    def c_(j):
        return rg("col", j, j + 1)
    KF, WT, DUM, KAP, CC, K16, TH, THS, KM, KMS, TO, TOS = [c_(j) for j in range(12)]
    E_ = [rg("Z", 15 - j, 143 - j) for j in range(16)]
    EW = [rg("Zw", 15 - j, 143 - j) for j in range(16)]
    F_ = [rg("FS", 128 * j, 128 * j + 128) for j in range(16)]
    D_ = [rg("DS", 128 * j, 128 * j + 128) for j in range(16)]
    G_ = [rg("GS", 128 * j, 128 * j + 128) for j in range(16)]
    Id, nI, n2I = rg("Id"), rg("nI"), rg("n2I")

    FX, BL = CO["FX"], CO["BL"]
    load(rg("z0b"), "z0", FX + 200)
    load(rg("cW"), "cb", FX + 200)
    load(rg("kai", 0, 1), "ka", FX + 200)
    load(rg("ADi", 0, 1024), "ad", FX + 0.5 * BL)
    load(rg("LEi"), "le", FX + BL)
    load(rg("VF", 0, 4096), "vf", FX + 2 * BL)
    load(rg("thi", 0, 1), "th", FX + 2 * BL)
    mset(rg("ones"), 1.0)
    iota(rg("pi", 0, 1), [[0, 1]], 0, 1)
    iota(rg("J16"), [[1, 16]], 0, 0)
    sel(rg("MRt"), rg("ones"), [[-16, 8], [0, 16]], ALU.is_ge, 0.0, 0, 1)
    sel(rg("BO"), rg("MRt"), [[16, 8], [0, 16]], ALU.is_ge, 0.0, 15, -1)
    sel(rg("Id"), rg("ones"), [[-1, 128]], ALU.is_equal, 0.0, 0, 1)
    ts(rg("ki", 0, 1), rg("pi", 0, 1), 15, ALU.bitwise_and)
    lin(KF, rg("ki", 0, 1))
    ts(rg("RMK"), rg("J16"), KF, ALU.is_equal)
    mset(rg("Z"), 0.0)
    lin(rg("Z", 15, 128, 16), rg("BO", 0, 128, 16))
    mset(rg("Zw"), 0.0)
    zw = rg("Zw", 15, 128, 16)
    iota(zw, [[-224, 8]], 1, 14)
    sel(zw, zw, [[-16, 8]], ALU.is_ge, 0.0, 0, 1)
    sel(zw, zw, [[16, 8]], ALU.is_ge, 0.0, 15, -1)
    for j in range(16):
        lin(F_[j], rg("BO"), rg("RMK", j, j + 1))
    for j in range(16):
        lin(D_[j], Id, rg("RMK", j, j + 1))
    lin(KAP, rg("kai", 0, 1), 1.0, 1184.0)
    ts(rg("kb", 0, 1), rg("kai", 0, 1), 15, ALU.bitwise_and)
    lin(CC, rg("kb", 0, 1), 2048.0)
    lin(TH, rg("thi", 0, 1), 1.0, 0.5)
    lin(THS, rg("thi", 0, 1), -256.0, -128.0)
    lin(KM, KF, 1.0, -3.5)
    lin(KMS, KF, 256.0, -896.0)
    lin(TO, rg("RMK", 0, 1), -2049.0, 0.5)
    lin(TOS, rg("RMK", 0, 1), -2049.0 * 256, 128.0)
    lin(DUM, KF, 1.0, 1024.0)
    lin(K16, KF, 16.0)
    for name, x in (("nI", -1.0), ("n2I", -2.0), ("nI64", -1.0 / 64), ("I32", 32.0), ("nI16", -16.0), ("nI4k", -4096.0)):
        lin(rg(name), Id, x)
    lin(rg("F32"), F_[15], 32.0)
    iota(rg("Ca"), [[16, 128]], -2048, 0)
    lin(rg("Ck"), rg("Ca"), 1.0, KF)
    for t0, t1 in PAR["mid"]:
        lin(rg("MS", 2 * t0, 2 * t0 + 128), F_[15], 10240.0 - 16 * t1)
    lin(rg("C2k"), rg("ones"), 2048.0)
    lin(rg("Cq"), rg("ones"), 0.25)
    sel(rg("TriI"), rg("BO"), [[1, 128]], ALU.is_ge, 0.0, 0, -1)
    iota(rg("MRt"), [[0, 8], [-1, 16]], 16, 0)
    lin(rg("MRt"), rg("MRt"), rg("RMK", 15, 16), -1.0)
    tt(rg("MR"), rg("MRt"), rg("BO"), ALU.mult)
    for t0, t1 in PAR["tail"]:
        lin(rg("T16", t0 // 16, t1 // 16), rg("J16", 0, (t1 - t0) // 16), 256.0, K16)
    act(rg("PL", 0, 2), rg("ones", 0, 2), AF.Sigmoid, 0.0, 256.0)
    ops[-1] = ops[-1][:5] + (ops[-1][5] + 1300, None)
    iota(rg("RX"), [[0, 64], [4096, 16]], 0, 0)
    iota(rg("RN"), [[0, 64], [-4096, 16]], 256, 0)
    iota(rg("RA"), [[0, 8], [8192, 16]], -2048, 0)
    lin(rg("RB"), rg("RN", 0, 256), 2.0 ** 88)
    sel(rg("HS"), rg("FS"), [[-1, 16], [0, 8], [1, 16]], ALU.is_gt, 0.0, 0, 0)
    sel(rg("GS"), rg("HS"), [[0, 16], [-1, 128]], ALU.not_equal, -1.0, 0, 1)
    lin(rg("MAt"), F_[15], -4096.0)
    sel(rg("MA1"), rg("MAt"), [[-1, 128]], ALU.not_equal, 4096.0, 0, 1)
    sel(rg("MA1"), rg("MA1"), [[-512, 8], [-33, 16]], ALU.not_equal, 0.0, 15, 32)
    sel(rg("MA2"), F_[15], [[-1, 128]], ALU.not_equal, -1.0, 1, 1)
    sel(rg("MA2"), rg("MA2"), [[-512, 8], [-31, 16]], ALU.not_equal, 0.0, 32, 32)
    lin(rg("LE", 0, 1024), rg("LEi"))

    def dedupe(t0, t1, place, xf, xval, sc, fd, mx, off):
        W = lambda n: rg(n, t0 // 16, t1 // 16)
        pd = ps(place, t0, t1)
        mm([(sub(pd, j, 16), G_[j], W(xf)) for j in range(16)], False)
        scan(rg(sc, t0, t1), rg("RB", 0, t1 - t0), pd, ALU.max, ALU.mult)
        ts(W(fd), rg(sc, t0 + 15, t1, 16), 0.0, ALU.is_equal, DUM, ALU.mult)
        if PAR["ttu"]:
            tt(rg(off, t0 // 8, t1 // 8, 2), W(fd), xval, ALU.max)
        else:
            tt(W(mx), W(fd), xval, ALU.max)
            lin(rg(off, t0 // 8, t1 // 8, 2), W(mx))

    for m in (1, 2, 3):
        last = m == 3
        zs = lambda a, b: rg("z0b", a, b) if m == 1 else rg("rcv%d" % m, 2 * a, 2 * b - 1, 2)
        As = lambda a, b: rg("rcv%d" % m, 2 * a + 1, 2 * b, 2)
        hh = lambda a, b: rg("snd1", 2 * a + 1, 2 * b, 2) if m == 1 else rg("hh", a, b)
        for t0, t1 in PAR["rc"][m]:
            n = t1 - t0
            W = lambda b: rg(b, t0 // 16, t1 // 16)
            L = lambda b: rg(b, t0, t1)
            wu, wb = rg("WF", t0 // 8, (t0 + t1) // 16), rg("WF", (t0 + t1) // 16, t1 // 8)
            pu = ps("u", t0, t1, 1, 16)
            mm([(pu, EW[j], sub(zs(t0, t1), j, 16)) for j in range(16)])
            lin(W("ui"), pu)
            ts(W("uu"), W("ui"), 4095, ALU.bitwise_and)
            lin(wu, W("uu"), 1.0, -2048.0)
            if m > 1:
                lin(W("c1"), W("uu"), 1103.0)
                ts(W("cW"), W("c1"), 4, ALU.arith_shift_right, 1023, ALU.bitwise_and)
            lin(W("c16"), W("cW"))
            lin(W("cf"), W("cW"), 1.0 / 1024, 1.0 / 1024)
            lin(W("b1"), W("cW"), 613.0)
            ts(W("b2"), W("b1"), 1023, ALU.bitwise_and)
            lin(wb, W("b2"), 32.0)
            pb = ps("D", t0, t1, 2)
            mm([(sub(pb, j, 16), F_[j], rg("WF", t0 // 8, t1 // 8)) for j in range(16)], False)
            lin(L("xf"), part(pb, 0, n), KAP, CC)
            tt(L("xa"), L("xf"), part(pb, n, 2 * n), ALU.add)
            ts(L("a32"), L("xa"), 5, ALU.arith_shift_right, 1023, ALU.bitwise_and)
            lin(L("a16"), L("a32"))
            for out in ("S16", "Sf"):
                lin(L(out), ind(rg("LEi" if m == 1 else "LE", 0, 1024), W("c16")))
        nb = 0
        for t0, t1 in PAR["mid"]:
            n = t1 - t0
            for q0, q1 in PAR["gat"]:
                if not t0 <= q0 < t1:
                    continue
                Q = lambda b: rg(b, q0, q1)
                B = lambda b: rg(b, 16 * q0, 16 * q1)
                sv = rg("VF", 8192 - 16 * (t1 + t0 - q0), 8192 - 16 * (t1 + t0 - q1))
                lin(sv, ind(rg("VF", 0, 4096), Q("S16")))
                lin(B("GA"), ind(rg("ADi", 0, 1024), Q("a16")), 1.0, -2048.0)
                pn = ps("C", q0, q1)
                mm([(pn, Id, rg("C2k", 0, q1 - q0))] + [(pn, D_[k], sub(B("GA"), k, 16)) for k in range(16)])
                lin(Q("n16"), pn)
                tt(B("AB"), ind(rg("VF", 0, 4096), Q("n16")), sv, ALU.subtract)
                for o in range(16 * q0, 16 * q1, PAR["abs"]):
                    act(rg("AB", o, min(o + PAR["abs"], 16 * q1)), rg("AB", o, min(o + PAR["abs"], 16 * q1)), AF.Abs)
            L = lambda b: rg(b, t0, t1)
            ab = rg("AB", 16 * t0, 16 * t1)
            pa, pb, pc = ps("A", t0, t1), ps("B", t0, t1), ps("C", t0, t1)
            tt(L("dn"), pc, L("Sf"), ALU.subtract)
            mm([(pa, E_[k], sub(ab, k, 16)) for k in range(16)] + [(pa, rg("nI64"), rg("C2k", 0, n))] * (m == 2)
               + ([(pa, rg("F32"), As(t0, t1))] if m > 1 else []))
            above(L("nok"), pa, TH, 1, THS)
            mm([(pb, rg("TriI"), L("nok"))])
            above(hh(t0, t1), pb, KM, -1, KMS)
            mm([(pa, rg("MR"), hh(t0, t1)), (pa, rg("I32"), L("nok"))])
            relu(L("vv"), pa, -16.0)
            mm([(pb, Id, rg("Ck", 0, n)), (pb, rg("MS", 2 * t0, 2 * t0 + 128), hh(t0, t1)), (pb, rg("nI16"), L("nok")), (pb, Id, L("vv"))])
            tt(L("p16"), pb, L("n16"), ALU.max)
            mm([(pc, Id, L("nok"))])
            tt(L("t1"), L("dn"), pc, ALU.mult)
            if m == 2:
                pq = ps("pa", t0, t1)
                mm([(pq, Id, hh(t0, t1)), (pq, Id, As(t0, t1))])
                lin(rg("snd2", 2 * t0 + 1, 2 * t1, 2), pq, 1.0, -2.0)
            if not last and t0 % 128 == 0:
                L = lambda b: rg(b, t0, t0 + 128)
                ab = rg("AB", 16 * t0, 16 * t0 + 2048)
                sd, pd, pe = ps("SD", t0, t0 + 128), ps("D", t0, t0 + 128), ps("E", t0, t0 + 128)
                mm([(sd, nI, rg("C2k"))] + [(sub(sd, k, 16), sub(ab, k, 16), rg("BO", 0, 128, 16)) for k in range(16)])
                scan(L("PM"), rg("RA"), sd, ALU.min, ALU.max)
                mm([(pd, L("PM"), Id)])
                lin(L("PL"), pd)
                mm([(pe, rg("MA1"), L("PL")), (pe, rg("MA2"), L("PL"))])
                above(L("noh"), pe, TO, -1, TOS)
                mm([(sd, Id, rg("ones")), (sd, nI, L("noh"))])
                tt(L("oa"), sd, L("a32"), ALU.mult)
        for t0, t1 in PAR["ddc"]:
            dedupe(t0, t1, "dc", "cf", rg("cW", t0 // 16, t1 // 16), "sc", "fdc", "mxc", "offc")
            for s in range(t1 // 16 - 1, t0 // 16 - 1, -1):
                tt(ind(rg("LE"), rg("offc", 2 * s, 2 * s + 1)), rg("Sf", 16 * s, 16 * s + 16), rg("t1", 16 * s, 16 * s + 16), ALU.add)
        if last:
            store("yl", 0, 1024, rg("LE", 0, 1024), FX + BW)
        else:
            for t0, t1 in PAR["dda"]:
                W = lambda b: rg(b, t0 // 16, t1 // 16)
                L = lambda b: rg(b, t0, t1)
                pw = ps("aw", t0, t1, 1, 16)
                mm([(pw, E_[j], sub(L("oa"), j, 16)) for j in range(16)])
                lin(W("a16W"), pw)
                lin(W("af"), pw, 1.0 / 1024, 1.0 / 1024)
                tt(L("keep"), ind(rg("ADi", 0, 1024), W("a16W")), L("noh"), ALU.mult)
                dedupe(t0, t1, "da", "af", pw, "sa", "fda", "mxa", "offa")
        tails, late = {a: b for a, b in PAR["tail"]}, []
        for t0, t1 in PAR["R"]:
            m0, m1 = [x for x in PAR["mid"] if x[0] <= t0 < x[1]][0]
            B = lambda b: rg(b, 16 * t0, 16 * t1)
            lin(B("WV"), ind(rg("VF", 0, 8192 - 16 * m0), rg("p16", t0, t1)))
            scan(B("HI"), rg("RX", 0, 16 * (t1 - t0)), B("WV"), ALU.min, ALU.max)
            scan(B("LO"), rg("RN", 0, 16 * (t1 - t0)), B("WV"), ALU.max, ALU.min)
            if t0 in tails:
                t1 = tails[t0]
                n = t1 - t0
                W = lambda b: rg(b, t0 // 16, t1 // 16)
                L = lambda b: rg(b, t0, t1)
                py = ps("A", t0, t1)
                mm([(py, n2I, rg("Cq", 0, n)), (py, n2I, zs(t0, t1)), (py, Id, rg("HI", 16 * t0 + 15, 16 * t1, 16)),
                    (py, Id, rg("LO", 16 * t0 + 15, 16 * t1, 16))])
                lin(L("y1"), py, 0.5, MAGIC)
                zn = L("zo") if last else rg("snd%d" % m, 2 * t0, 2 * t1 - 1, 2)
                act(zn, L("y1"), AF.Abs, -MAGIC)
                if not last:
                    snd, rcv, sem = "snd%d" % m, "rcv%d" % (m + 1), "arr%d%d" % (m, t0 // 32)
                    bs = [b for b in range(t0 // 32, t1 // 32) if (b + m) % 8]
                    tok = ("tok", 8 * m + t0 // 32, 8 * m + t0 // 32 + 1, 1)
                    share = n // 32
                    if bs:
                        add("G", "send", (snd, rcv, bs, m, sem, share), [rg(snd, 2 * t0, 2 * t1)], [tok], CO["SND"])
                        add("X", "arr", (sem, len(bs), share), [tok], [rg(rcv, 64 * b, 64 * b + 64) for b in bs], CO["ARR"] + 250 * share)
                    for b in range(t0 // 32, t1 // 32):
                        if (b + m) % 8 == 0:
                            dma("lcp", (rg(rcv, 64 * b, 64 * b + 64), rg(snd, 64 * b, 64 * b + 64)), [rg(snd, 64 * b, 64 * b + 64)],
                                [rg(rcv, 64 * b, 64 * b + 64)], 2000)
                pu = ps("w", t0, t1, 1, 16)
                mm([(pu, EW[j], sub(zn, j, 16)) for j in range(16)])
                lin(W("wi"), pu)
                ts(W("wl"), W("wi"), 15, ALU.bitwise_and)
                tt(W("w16"), W("wl"), W("T16"), ALU.add)
                if not last:
                    lin(W("wp"), W("w16"), 1.0, 16.0 * t0 - 2048.0)
                late.append((t0, t1, zn))
                if last and t0 % 128 == 0:
                    store("yz", t0, t0 + 128, rg("zo", t0, t0 + 128), FX + 300)
                if not last:
                    pb = ps("B", t0, t1)
                    mm([(pb, Id, rg("C2k", 0, n)), (pb, rg("nI4k"), L("noh"))] + [(sub(pb, j, 16), F_[j], W("wp")) for j in range(16)])
                    tt(L("nw"), L("keep"), pb, ALU.max)
                    for s in range(t1 // 16 - 1, t0 // 16 - 1, -1):
                        cp(ind(rg("ADi"), rg("offa", 2 * s, 2 * s + 1)), rg("nw", 16 * s, 16 * s + 16))
        for t0, t1, zn in late:
            vf = rg("VF", 16 * t0, 16 * t1)
            cp(ind(vf, rg("w16", t0 // 16, t1 // 16)), zn)
            if last:
                store("yv", 16 * t0, 16 * t1, vf, FX + BW * (t1 - t0) / 128)
    return ops


def overlap(a, b):
    la = a[1] + (cnt(a) - 1) * a[3]
    lb = b[1] + (cnt(b) - 1) * b[3]
    return a[1] <= lb and b[1] <= la


def depend(ops):
    hist, anc, red = {}, [], []
    for i, o in enumerate(ops):
        d = set()
        for kind, regs in ((0, o[3]), (1, o[4])):
            for r in set(regs):
                for (j, k2, r2) in hist.get(r[0], []):
                    if (kind or k2) and overlap(r, r2):
                        d.add(j)
        for kind, regs in ((0, o[3]), (1, o[4])):
            for r in set(regs):
                hist.setdefault(r[0], []).append((i, kind, r))
        a = 0
        for j in d:
            a |= anc[j]
        red.append(sorted(j for j in d if not (a >> j) & 1))
        for j in d:
            a |= 1 << j
        anc.append(0 if o[0] == "X" else a)
    return red


EI = {e: k for k, e in enumerate("VAPGSX")}


def replay(order, eng, cost, deps, banks, lat, a=0, old=None):
    n = len(order)
    free, lastop = [0.0] * 6, [None] * 6
    b1, b2 = [None] * 8, [None] * 8
    if a:
        fin, why = list(old[0]), list(old[1])
        for i in order[:a]:
            e = eng[i]
            lastop[e] = i
            for b in banks[i]:
                j = b1[b]
                if j is not None and eng[j] != e:
                    b2[b] = j
                b1[b] = i
        for e in range(4):
            if lastop[e] is not None:
                free[e] = fin[lastop[e]]
        if lastop[4] is not None:
            free[4] = fin[lastop[4]] - cost[lastop[4]] + 60.0
        lastop[4] = lastop[5] = None
    else:
        fin, why = [0.0] * n, [None] * n
    for i in order[a:]:
        e = eng[i]
        s, w = free[e], lastop[e]
        if w is not None:
            w = ~w
        for j in deps[i]:
            t = fin[j] + lat
            if t > s:
                s, w = t, j
        for b in banks[i]:
            j = b1[b]
            if j is not None and eng[j] != e:
                b2[b] = j
            else:
                j = b2[b]
            b1[b] = i
            if j is not None:
                t = fin[j] + lat
                if t > s:
                    s, w = t, ~j
        f = s + cost[i]
        fin[i], why[i] = f, w
        if e < 4:
            free[e], lastop[e] = f, i
        elif e == 4:
            free[4] = s + 60.0
    return fin, why


def listed(deps, succ, banks, opt, dl, lat, wait, lean):
    n = len(deps)
    left = [len(d) for d in deps]
    at = [0.0] * n
    rdy = [i for i in range(n) if not left[i]]
    free, bf = [0.0] * 6, [[0.0] * 3 for _ in range(8)]
    order, pick, end = [], [0] * n, 0.0
    while rdy:
        cands, s0, e0 = [], 1e18, 0
        for i in rdy:
            bv = 1e18
            for e, c, k in opt[i]:
                s = at[i]
                if free[e] > s:
                    s = free[e]
                for b in banks[i]:
                    x = bf[b]
                    for e2 in range(3):
                        if e2 != e and x[e2] > s:
                            s = x[e2]
                v = s + c + (lean if e == 0 else 0.0)
                if v < bv:
                    best, bv = (s, e, i, k, c), v
            cands.append(best)
            if best[0] < s0:
                s0, e0 = best[:2]
        bk = 1e18
        for x in cands:
            if x[1] == e0 and dl[x[2]] + wait * (x[0] - s0) < bk:
                bk, bx = dl[x[2]] + wait * (x[0] - s0), x
        s, e, i, k, c = bx
        rdy.remove(i)
        order.append(i)
        pick[i], f = k, s + c
        if f > end:
            end = f
        if e < 4:
            free[e] = f
        elif e == 4:
            free[e] = s + 60.0
        for b in banks[i]:
            bf[b][e] = f + lat
        for j in succ[i]:
            if f + lat > at[j]:
                at[j] = f + lat
            left[j] -= 1
            if not left[j]:
                rdy.append(j)
    return end, order, pick


def improve(ops, deps, banks, order, pick, scen, iters, rnd):
    n = len(ops)

    def tabs(pick):
        return ([EI[ops[i][6][0] if pick[i] else ops[i][0]] for i in range(n)],
                [[so[i][6][3] if pick[i] else so[i][5] for i in range(n)] for so, _l, _w in scen])

    def ev(order, tb, a, olds):
        res = [replay(order, tb[0], tb[1][k], deps, banks, scen[k][1], a, olds and olds[k]) for k in range(len(scen))]
        return sum(scen[k][2] * max(r[0]) for k, r in enumerate(res)), res
    tb = tabs(pick)
    cur, res = ev(order, tb, 0, None)
    best = (cur, order, pick)
    for it in range(iters):
        temp = PAR["temp"] * (1.0 - it / iters) + 5.0
        fin, why = res[int(rnd() * len(scen))]
        arcs, i = [], fin.index(max(fin))
        while i is not None:
            w = why[i]
            if w is not None and w < 0:
                w = ~w
                arcs.append((w, i))
            i = w
        no, npk = order, pick
        r = rnd()
        if r < 0.2 or not arcs:
            on = [x for a in arcs for x in a if ops[x][6]]
            if not on:
                continue
            f = on[int(rnd() * len(on))]
            npk = list(pick)
            npk[f] ^= 1
            a = order.index(f)
            ch = [f]
            if rnd() < 0.4:
                near = [x for x in order[a + 1:a + 40] if ops[x][6] and tb[0][x] != tb[0][f] and abs(ops[x][5] - ops[f][5]) < 200]
                if near:
                    ch.append(near[int(rnd() * len(near))])
                    npk[ch[1]] ^= 1
            ntb = (list(tb[0]), [list(c) for c in tb[1]])
            for x in ch:
                ntb[0][x] = 1 - ntb[0][x]
                for k, c in enumerate(ntb[1]):
                    c[x] = scen[k][0][x][6][3] if npk[x] else scen[k][0][x][5]
        else:
            ntb = tb
            k = int(rnd() * len(arcs))
            u, v = arcs[k]
            while rnd() < 0.5 and k + 1 < len(arcs) and arcs[k + 1][1] == u:
                k += 1
                u = arcs[k][0]
            a, b = order.index(u), order.index(v)
            seg = order[a:b + 1]
            if r < 0.6:
                need = {v}
                for x in reversed(seg):
                    if x in need:
                        need.update(deps[x])
                if u in need:
                    continue
                seg = [x for x in seg if x in need] + [x for x in seg if x not in need]
            else:
                aft = {u}
                for x in seg:
                    if any(j in aft for j in deps[x]):
                        aft.add(x)
                if v in aft:
                    continue
                seg = [x for x in seg if x not in aft] + [x for x in seg if x in aft]
            no = order[:a] + seg + order[b + 1:]
        val, nres = ev(no, ntb, a, res)
        if val <= cur or rnd() < 2.718281828 ** ((cur - val) / temp):
            cur, pick, res, tb, order = val, npk, nres, ntb, no
            if it % 8 == 0:
                f0, c0 = res[0][0], tb[1][0]
                order = sorted(no, key=lambda x: round(f0[x] - c0[x], 3))
            if cur < best[0]:
                best = (cur, order, pick)
    return best


def place(seq, a, old, deps, banks, eng, cost, lat):
    st = list(old)
    lo, hi = [[] for _ in range(4)], [[] for _ in range(4)]
    bk = [[] for _ in range(8)]
    for i in seq[:a]:
        e = eng[i]
        if e < 4:
            lo[e].append(st[i])
            hi[e].append(st[i] + cost[i])
            for b in banks[i]:
                bk[b].append((st[i], st[i] + cost[i], e))
    for i in seq[a:]:
        t, e, c = 0.0, eng[i], cost[i]
        for j in deps[i]:
            x = st[j] + cost[j] + lat
            if x > t:
                t = x
        if e < 4:
            L, H = lo[e], hi[e]
            k = len(L)
            while k and H[k - 1] > t:
                k -= 1
            moved = True
            while moved:
                moved = False
                while k < len(L) and L[k] < t + c:
                    if H[k] > t:
                        t = H[k]
                    k += 1
                for b in banks[i]:
                    B = bk[b]
                    q = len(B) - 1
                    while q >= 0 and B[q][0] + 1500.0 > t:
                        x, y, e2 = B[q]
                        if e2 != e and x < t + c + lat and y + lat > t:
                            t, moved = y + lat, True
                            break
                        q -= 1
            L.insert(k, t)
            H.insert(k, t + c)
            for b in banks[i]:
                B = bk[b]
                q = len(B)
                while q and B[q - 1][0] > t:
                    q -= 1
                B.insert(q, (t, t + c, e))
        st[i] = t
    return st


def refine(ops, slow, deps, banks, order, pick, iters, rnd):
    n, lat = len(ops), CO["LAT"]
    pick = list(pick)
    eng = [EI[o[6][0] if pick[i] else o[0]] for i, o in enumerate(ops)]
    cost = [o[6][3] if pick[i] else o[5] for i, o in enumerate(ops)]
    flex = [i for i in range(n) if ops[i][6]]
    big = [i for i in flex if ops[i][5] > 600]

    cost2 = [o[6][3] if pick[i] else o[5] for i, o in enumerate(slow)]

    def value(st):
        fin = [st[i] + cost[i] for i in range(n)]
        sq = sorted(range(n), key=lambda i: (st[i], i))
        fin2 = replay(sq, eng, cost2, deps, banks, lat)[0]
        end = max(fin) + PAR["even"] * max(fin2)
        return end + PAR["pull"] * (sum(fin) + PAR["even"] * sum(fin2)) / n, end, sq

    def flip(xs):
        for x in xs:
            pick[x] ^= 1
            eng[x] = 1 - eng[x]
            cost2[x] = slow[x][6][3] if pick[x] else slow[x][5]
            cost[x] = ops[x][6][3] if pick[x] else ops[x][5]
    st = place(order, 0, [0.0] * n, deps, banks, eng, cost, lat)
    cur, end, seq = value(st)
    best = (end, seq, list(pick))
    for it in range(iters):
        temp = PAR["heat"] * (1.0 - it / iters) + 3.0
        r, ch = rnd(), []
        if r < 0.25:
            pool = big if rnd() < 0.3 else flex
            ch = [pool[int(rnd() * len(pool))]]
            if rnd() < 0.5:
                i = ch[0]
                near = [j for j in flex if eng[j] != eng[i] and abs(st[j] - st[i]) < 2000 and abs(cost[j] - cost[i]) < 300]
                if near:
                    ch.append(near[int(rnd() * len(near))])
            flip(ch)
            ns, a = seq, min(seq.index(x) for x in ch)
        else:
            i, d = int(rnd() * n), 3000.0 * abs(rnd() + rnd() - 1.0)
            pr = list(st)
            if r < 0.65:
                stack, seen = [i], {i}
                while stack:
                    x = stack.pop()
                    pr[x] -= d
                    for j in deps[x]:
                        if j not in seen and st[j] > st[i] - 2500.0:
                            seen.add(j)
                            stack.append(j)
            else:
                pr[i] += d
            for x in range(n):
                for j in deps[x]:
                    if pr[j] >= pr[x]:
                        pr[x] = pr[j] + 1e-3
            ns = sorted(range(n), key=lambda i: pr[i])
            a = 0
            while a < n and ns[a] == seq[a]:
                a += 1
            if a == n:
                continue
        s2 = place(ns, a, st, deps, banks, eng, cost, lat)
        v, end, sq = value(s2)
        if v <= cur or rnd() < 2.718281828 ** ((cur - v) / temp):
            cur, st, seq = v, s2, sq
            if end < best[0]:
                best = (end, seq, list(pick))
        else:
            flip(ch)
    return best


PLAN = {}
SCEN = [({}, 0.6), ({"CY": 1.2, "PCY": 0.6, "GC": 2.0, "SCT": 5.3}, 0.4)]


def plan():
    if not PLAN:
        base, scen = dict(CO), []
        for sc, w in SCEN:
            CO.update(sc)
            scen.append((build(), CO["LAT"], w))
            CO.update(base)
        ops = scen[0][0]
        n = len(ops)
        deps = depend(ops)
        banks = [sorted(set(int(r[0][1:]) for r in o[3] + o[4] if isps(r))) for o in ops]
        succ = [[] for _ in range(n)]
        for i in range(n):
            for j in deps[i]:
                succ[j].append(i)
        st = [PAR["seed"]]

        def rnd():
            st[0] = (st[0] * 6364136223846793005 + 1442695040888963407) % 18446744073709551616
            return (st[0] >> 11) / 9007199254740992.0
        big, seen = {}, {}
        for i, o in enumerate(ops):
            if o[0] in "VA" and isinstance(o[2][1], list) and o[4][0][0] in ("VF", "AB", "GA", "WV"):
                nm = {"S16": "S", "a16": "G", "n16": "N", "p16": "R"}[o[2][1][2][0]]
                per = len(PAR["R" if nm == "R" else "gat"])
                seen[nm] = seen.get(nm, -1) + 1
                big[i] = (seen[nm] // per, nm + str(seen[nm] % per))
        due = {(m, w[:2]): (1000.0 * float(w[4:]), EI[w[2]]) for m in range(3) for w in PAR["due"][m].split()}
        for m, k in sorted(big.values()):
            if (m, k) not in due:
                t, e = due[(m, k[0] + str(int(k[1]) - 1))]
                due[(m, k)] = (t + 1000.0, e)
        keys = sorted(set(k[1] for k in big.values()))
        both = [[(EI[o[0]], o[5], 0)] + ([(EI[o[6][0]], o[6][3], 1)] if o[6] else []) for o in ops]

        def ev(due):
            dl, opt = [0.0] * n, list(both)
            for i in range(n - 1, -1, -1):
                if i in big:
                    dl[i] = big[i][0] * PAR["step"] + due[big[i]][0]
                    opt[i] = [x for x in both[i] if x[0] == due[big[i]][1]] or both[i]
                else:
                    dl[i] = min([dl[j] for j in succ[i]] + [3 * PAR["step"] + 3000.0]) - ops[i][5] - CO["LAT"]
            end, order, pick = listed(deps, succ, banks, opt, dl, CO["LAT"], PAR["wait"], PAR["lean"])
            eng = [both[i][pick[i]][0] for i in range(n)]
            cost2 = [o[6][3] if pick[i] else o[5] for i, o in enumerate(scen[1][0])]
            return end + PAR["even"] * max(replay(order, eng, cost2, deps, banks, CO["LAT"])[0]), order, pick
        cur = best = ev(due)
        PLAN["due"] = due
        for it in range(PAR["tries"]):
            nd = dict(due)
            for _ in range(1 + int(3 * rnd())):
                k, d, flip = keys[int(rnd() * len(keys))], 5000.0 * (rnd() + rnd() - 1.0), rnd() < 0.35
                for m in (range(3) if rnd() < 0.3 else [int(3 * rnd())]):
                    t, e = nd[(m, k)]
                    nd[(m, k)] = (t, 1 - e) if flip else (t + d, e)
            v = ev(nd)
            if v[0] <= cur[0] + 300.0 * rnd():
                cur, due = v, nd
                if v[0] < best[0]:
                    best = v
                    PLAN["due"] = due
        val, order, pick = refine(ops, scen[1][0], deps, banks, best[1], best[2], PAR["iters"], rnd)
        ops = [o[6][:3] + o[3:5] + (o[6][3], None) if pick[i] else o for i, o in enumerate(ops)]
        PLAN["p"] = (ops, deps, banks, order, val, pick, best[0])
    return PLAN["p"]


def rank_program(g, core, T, topo):
    rank = T.rank_of(core)
    if rank is None:
        return
    ops, deps, banks, order = plan()[:4]
    Q = {"V": g.vector, "A": g.scalar, "P": g.tensor, "G": g, "S": g.sync}

    def ap(x):
        if isinstance(x, list):
            return ap(x[1]).indirect(ap(x[2]))
        if isinstance(x, tuple):
            return T[x[0]][:, x[1]:x[2]:x[3]] if x[3] != 1 else T[x[0]][:, x[1]:x[2]]
        return x

    pos = {i: k for k, i in enumerate(order)}
    known, done, waits, user = {e: 0 for e in Q}, {}, {}, [{} for _ in range(8)]
    ran = {e: 0 for e in Q}
    for i in order:
        e = ops[i][0]
        if e == "X":
            done[i] = 1 << i
            continue
        need = set(deps[i])
        for b in banks[i]:
            need.update(j for e2, j in user[b].items() if e2 != e)
            user[b][e] = i
        waits[i] = []
        for j in sorted(need, key=lambda x: -pos[x]):
            if not (known[e] >> j) & 1:
                waits[i].append(j)
                known[e] |= done[j]
        if e == "S" or ops[i][1] == "send":
            done[i] = known[e] | 1 << i
        else:
            ran[e] |= known[e] | 1 << i
            done[i] = ran[e]
    sig, count, total = {}, {}, {}
    for i in order:
        e, kind, a = ops[i][:3]
        if e == "S":
            sig[i] = (a[-1], 16)
        elif kind == "arr":
            src = T.cores[(rank + 1) % len(T.cores)]
            sig[i] = (a[0], a[1] * (len(topo.engines(src, core)) // a[2]))
        elif kind != "send":
            count[e] = count.get(e, 0) + 1
            sig[i] = ("s" + e, count[e])
        if i in sig:
            total[sig[i][0]] = sig[i][1]
    sent = 0
    for i in order:
        e, kind, a = ops[i][:3]
        if e == "X":
            continue
        q = Q[e]
        for j in waits[i]:
            q.wait_ge(T.sem[sig[j][0]], sig[j][1])
        if kind == "cp":
            ins = q.tensor_copy(ap(a[0]), ap(a[1]))
        elif kind == "ts":
            if a[5] is None:
                ins = q.tensor_scalar(ap(a[0]), ap(a[1]), ap(a[2]), None, a[4])
            else:
                ins = q.tensor_scalar(ap(a[0]), ap(a[1]), ap(a[2]), ap(a[3]), a[4], a[5])
        elif kind == "tt":
            ins = q.tensor_tensor(ap(a[0]), ap(a[1]), ap(a[2]), a[3])
        elif kind == "scan":
            ins = q.tensor_tensor_scan(ap(a[0]), ap(a[1]), ap(a[2]), 0.0, a[3], a[4])
        elif kind == "mset":
            ins = q.memset(ap(a[0]), a[1])
        elif kind == "act":
            ins = q.activation(ap(a[0]), ap(a[1]), a[2], bias=ap(a[3]), scale=ap(a[4]))
        elif kind == "mm":
            for k, (o, l, r) in enumerate(a[0]):
                ins = q.matmul(ap(o), ap(l), ap(r), k == 0 or not a[1], k == len(a[0]) - 1 or not a[1])
        elif kind == "iota":
            if SB[a[0][0]][1] == I32:
                ins = q.iota(ap(a[0]), a[1], a[2], a[3])
            else:
                ins = q.iota(ap(a[0]), a[1], a[2], a[3], allow_small_or_imprecise_dtypes=True)
        elif kind == "sel":
            ins = q.affine_select(ap(a[0]), ap(a[1]), a[2], a[3], a[4], a[5], a[6])
        elif kind == "load":
            ins = q.dma_start(ap(a[0]), T[a[1]][:])
        elif kind == "store":
            ins = q.dma_start(T[a[0]][:, a[1]:a[2]], ap(a[3]))
        elif kind == "lcp":
            ins = q.dma_start(ap(a[0]), ap(a[1]))
        elif kind == "send":
            trs = []
            for k, b in enumerate(a[2]):
                dst = T.cores[(rank + b + a[3]) % len(T.cores)]
                rid, pid = topo.addr(dst)[:2]
                en = topo.engines(core, dst)
                w = len(en) // a[5]
                mask = sum(1 << x for x in en[k * w:(k + 1) * w])
                trs.append(RemoteDMATransfer(dst_ids=[DstId(rid=rid, pnc=pid)], dma_engine_mask=mask, remote_sem=T.sem[a[4]],
                                             src=T[a[0]][:, 64 * b:64 * b + 64], dst=T[a[1]][:, 64 * b:64 * b + 64]))
                sent += w
            g.remote_dma_fused(trs, local_sem=T.sem.snt)
            continue
        ins.then_inc(T.sem[sig[i][0]], 16 if e == "S" else 1)
    total["snt"] = sent
    for s, v in total.items():
        g.wait_ge(T.sem[s], v)
